import numpy as np, ml_dtypes
CORES = [6,15,38,47]
N = 4
BF = ml_dtypes.bfloat16
def gentries(a):
    return np.ascontiguousarray(a.reshape(8, 16, -1).transpose(0, 2, 1)).reshape(8, -1)
def gtable(e):
    e = np.asarray(e); return np.ascontiguousarray(e.reshape(8, -1, 16).transpose(0, 2, 1)).reshape(128, -1).astype(np.int32)
P, L, S, F, RO = 4096, 4096, 4, 256, 2
H = P - F
def depths(rng, up, top):
    s = np.where(rng.random((N, 8, P)) < up, 1, 1 - rng.geometric(0.5, (N, 8, P))); d = np.zeros((N, 8, P), np.int64); now = np.zeros((N, 8), np.int64)
    for v in range(1, P):
        now = np.minimum(np.maximum(now + s[:, :, v], 0), top); d[:, :, v] = now
    return d
def closed(d):
    e = np.zeros(d.shape, np.int64); last = np.full(d.shape[:-1] + (1,), P, np.int64)
    for k in range(int(np.max(d)) + 1):
        m = np.minimum.accumulate(np.where(d <= k, np.arange(P), P)[..., ::-1], axis=-1)[..., ::-1]
        e = np.where(d == k, np.concatenate([m[..., 1:], last], axis=-1), e)
    return e
def parts(rng):
    up = rng.choice(np.array([0.4, 0.5, 0.6]), (N, 8, 1)); top = rng.integers(3, 13, (N, 8))
    full = np.arange(P) < (P * rng.choice(np.array([8, 12, 14, 16]), (N, 8, 1))) // 16
    d = np.where(full, depths(rng, up, top), 0)
    x = np.where(rng.random((N, 8, 16, P)) < 0.25, rng.integers(0, 4, (N, 8, 16, P)), rng.integers(0, 256, (N, 8, 16, P))) * full[:, :, None, :]
    return x, d, rng.integers(0, 256, (N, 8, 16, L)), rng.integers(0, P, (N, 8, RO, L))
def pack(x, e, w, st):
    return {"x": np.ascontiguousarray(x.reshape(N, 128, P)).astype(np.float32).astype(BF), "w": np.ascontiguousarray(w.reshape(N, 128, L)).astype(np.float32).astype(BF),
            "ends": np.ascontiguousarray(e).astype(np.int32), "start": np.stack([gtable(a.reshape(8, -1)) for a in st])}
def setup_inputs(rng):
    x, d, w, st = parts(rng)
    return pack(x, closed(d), w, st)
def setup_inputs_room(rng):
    x, d, w, st = parts(rng); x = rng.integers(0, 256, x.shape); Q = P // 16; z = F // 4
    at = ((H - z, H), (H - z + 1, H + 1), (H, H + z), (H - 1, H - 1 + z), (P - z, P), (P - z + 1, P + 1), (P - 1, P - 1 + z), (H - z, -1))
    for q in range(N):
        for g in range(8):
            n = int(rng.integers(Q // 2, Q + 1)); a, b = at[(g + q) % 8]; a = a - n; b = P if b < 0 else b - n; D = d[q, g].copy()
            d[q, g] = np.concatenate([np.tile(np.arange(3), Q), D[:a - 3 * Q], np.zeros(1, np.int64), 1 + D[:b - a - 1], D[:P - b]])
            hot = 3 * rng.permutation(Q)[:n]
            st[q, g, 0] = rng.permutation(np.concatenate([hot, rng.choice(hot, L - n)]))
    return pack(x, closed(d), w, st)
def setup_inputs_ties(rng):
    x, d, w, st = parts(rng); lo = rng.choice(np.array([0, 100, 252]), (N, 8, 1, 1))
    x = lo + rng.integers(0, 4, x.shape); x[:, 1::2] = (lo + 2 * rng.integers(0, 2, (N, 8, 1, P)))[:, 1::2]
    return pack(x, closed(d), np.minimum(lo + rng.integers(0, 5, w.shape), 255), st)
def setup_inputs_alike(rng):
    x, d, w, st = parts(rng); x = rng.integers(0, 256, x.shape); e = closed(d); at = np.arange(P)
    names = rng.integers(0, P, (N, 8, RO, 6)); names[..., 0] = 0; names[..., 1] = P - 1
    st = np.take_along_axis(names, rng.integers(0, 6, st.shape), 3)
    for q in range(N):
        g = (np.arange(4) + q) % 8
        e[q, g[0]] = P; st[q, g[0], 0] = rng.choice(np.array([0, P - 1, P - 2, P - 3, P - 1 - S, P - 2 - S]), L)
        e[q, g[1]] = at + 1; e[q, g[1], :2] = P; st[q, g[1], 0] = 0
        e[q, g[2]] = at + 1
        e[q, g[3]] = np.where(at % 2 == 0, P, at + 1); st[q, g[3], 0] = rng.integers(0, P, L)
    return pack(x, e, w, st)
def setup_inputs_far(rng):
    x, d, w, st = parts(rng); x = rng.integers(0, 256, x.shape); w = rng.integers(1, 256, w.shape); g = rng.permutation(8); odd = np.arange(N) % 2 == 1; i4 = np.arange(16)[:, None] % 4
    kid = np.where(odd, rng.integers(3 * P // 4 + 2, P - 1, N), P - 1); low = np.where(odd, rng.integers(3 * P // 4, H, N), P - 1)
    left = np.where(odd, rng.integers(15 * P // 32, P // 2 - 4, N), rng.integers(7 * P // 16 + 1, 15 * P // 32, N)); T = min(P // 7, L // 4)
    st[:, g[:4]] = P - 1
    for q in range(N):
        D = d[q].copy(); b = int(kid[q]); z = int(low[q]); s = int(left[q]); m = D[g[0]]
        d[q, g[0]] = np.concatenate([np.array([0, 1, 2, 3]), 3 + m[:b - 4], np.array([2]), m[:P - b - 1]])
        x[q, g[0], :, b] = 0; st[q, g[0], 0] = 0
        d[q, g[1]] = np.concatenate([np.zeros(z + 1, np.int64), D[g[1]][:P - z - 1]])
        v = rng.choice(np.array([0, z - 2]), L); v[0] = 0; v[1] = z - 2; st[q, g[1], 0] = v
        m = D[g[2]]; d[q, g[2]] = np.concatenate([np.arange(3), 2 + m[:s - 1], m[:P - s - 2]]); st[q, g[2], 0] = 0
        m = D[g[3]]; a = H - 4 + q % 2
        d[q, g[3]] = np.concatenate([m[:H - 4], np.array([0, 0, 1, 2, 3]) if q % 2 else np.array([0, 1, 2, 3, 3]), m[:P - H - 1]])
        v = np.where(rng.random(L) < 0.5, a, rng.integers(H, P, L)); v[0] = a; st[q, g[3], 1] = v
        d[q, g[4]] = np.concatenate([np.tile(np.array([0, 1, 2, 2, 1, 2, 2]), T), D[g[4]][:P - 7 * T]])
        few = np.array([4, 0, 2, 3, 1, 2, 3])[np.arange(P) % 7]
        x[q, g[4]] = np.where(i4 == few, rng.integers(0, 61, (16, P)), rng.integers(200, 256, (16, P)))
        j = rng.permutation(np.concatenate([np.arange(4 * T), rng.integers(0, 4 * T, L - 4 * T)])); st[q, g[4], 0] = 7 * (j // 4)
        w[q, g[4]] = np.where((i4 == (j % 4) // 2) | (i4 == 2 + j % 2), rng.integers(100, 201, (16, L)), 0)
    x[:, g[0], :, 2] = 255; x[:, g[0], :, 3] = 0; x[:, g[0], :, 4] = 255; x[:, g[3], :, H - 1] = 255; x[:, g[3], :, H] = 0
    for k in (1, 2):
        x[:, g[k], :, 2] = 0; x[:, g[k], :, 3] = 255
    e = closed(d)
    for q in range(N):
        z = int(low[q]); e[q, g[1], :z + 1] = z + 1; e[q, g[1], 2] = 3
    return pack(x, e, w, st)
def setup_inputs_spread(rng):
    x, d, w, st = parts(rng)
    d = depths(rng, 0.35 + 0.35 * rng.random((N, 8, 1)), np.exp2(1 + 5 * rng.random((N, 8))).astype(np.int64) + 1)
    x = np.minimum((np.exp2(8 * rng.random((N, 8, 1, P))) * rng.random((N, 8, 16, P))).astype(np.int64), 255)
    w = np.minimum((np.exp2(8 * rng.random((N, 8, 1, L))) * rng.random((N, 8, 16, L))).astype(np.int64), 255)
    st = np.minimum((P * rng.random((N, 8, RO, L)) ** rng.choice(np.array([1, 2, 4]), (N, 8, 1, 1))).astype(np.int64), P - 1)
    return pack(x, closed(d), w, st)
def check_inputs(d):
    bad = []
    for k in ("x", "w"):
        v = d[k].astype(np.float32)
        if not np.all((v >= 0) & (v <= 255) & (v == np.floor(v))): bad.append("whole numbers from 0 to 255 in " + k)
    e = d["ends"].astype(np.int64); n = e - np.arange(P)
    if np.min(n) < 1 or np.max(e) > P: bad.append("range of ends")
    else:
        big = e; most = np.zeros(e.shape, np.int64); k = 1
        while k <= P:
            sel = (n >= k) & (n < 2 * k)
            most = np.where(sel, np.maximum(big, np.take_along_axis(big, np.where(sel, e - k, 0), 2)), most)
            big = np.concatenate([np.maximum(big[..., :P - k], big[..., k:]), big[..., P - k:]], axis=2); k = 2 * k
        if np.any(most > e): bad.append("runs that cross")
    if np.min(d["start"]) < 0 or np.max(d["start"]) > P - 1: bad.append("range of start")
    return bad
def grow(x, e, w, v):
    G = np.arange(8)[:, None]; at = np.arange(P); n = np.zeros((8, L), np.int64); par = v
    for i in range(S):
        ev = e[G, v]; a = np.minimum(v + 1, P - 1); b = e[G, a]; kids = ev > v + 1; two = kids & (b < ev); b = np.minimum(b, P - 1)
        ra = np.add.reduce(np.maximum(w - x[G, a], 0), axis=2); rb = np.add.reduce(np.maximum(w - x[G, b], 0), axis=2)
        par = np.where(kids, v, par); n = n + kids; v = np.where(kids, np.where(two & (rb > ra), b, a), v)
    hit = (n >= 2) & (e[G, v] == v + 1); gi = np.broadcast_to(G, v.shape)[hit]
    head = np.zeros((8, P), bool); head[gi, v[hit]] = True; mark = np.zeros((8, P), bool); mark[gi, par[hit]] = True
    zero = np.zeros((8, 1), np.int64); reach = np.maximum.accumulate(np.where(mark, e, 0), axis=1)
    top = mark & (np.concatenate([zero, reach[:, :-1]], axis=1) <= at); inside = reach > at; keep = ~head
    first = np.maximum.accumulate(np.where(top, at, 0), axis=1)
    K = np.concatenate([zero, np.add.accumulate(keep.astype(np.int64), axis=1)], axis=1)
    M = np.concatenate([zero, np.add.accumulate(keep * (1 + 2 * inside), axis=1)], axis=1)
    size = np.where(inside, K[G, e] - K[:, :P], M[G, e] - M[:, :P]); s = K[G, e[G, first]] - K[G, first]
    nx = np.zeros((8, P, 16), np.int64); ne = np.zeros((8, P), np.int64) + at + 1
    for c in range(3):
        q = np.where(inside, M[G, first] + c * s + K[:, :P] - K[G, first], M[:, :P])
        gk, vk = np.nonzero(keep & (inside | (c == 0)) & (q < P)); qk = q[gk, vk]
        nx[gk, qk] = np.maximum(x[gk, vk] - c, 0); ne[gk, qk] = qk + size[gk, vk]
    return nx, ne
def reference(x, w, ends, start):
    X = np.ascontiguousarray(x.astype(np.float32).astype(np.int64).reshape(N, 8, 16, P).transpose(0, 1, 3, 2)); E = ends.astype(np.int64)
    W = np.ascontiguousarray(w.astype(np.float32).astype(np.int64).reshape(N, 8, 16, L).transpose(0, 1, 3, 2))
    st = np.stack([gentries(a) for a in start]).astype(np.int64).reshape(N, 8, RO, L)
    for t in range(RO):
        both = [grow(X[r], E[r], W[r], st[r, :, t]) for r in range(N)]
        gx = np.stack([a for a, b in both]); ge = np.stack([b for a, b in both])
        X = np.concatenate([gx[:, :, :H], np.roll(gx[:, :, H:], 1, axis=0)], axis=2)
        E = np.concatenate([np.minimum(ge[:, :, :H], H), np.roll(np.minimum(ge[:, :, H:], P), 1, axis=0)], axis=2)
    return {"y": np.ascontiguousarray(X.transpose(0, 1, 3, 2)).reshape(N, 128, P).astype(np.float32).astype(BF), "ye": E.astype(np.float32)}

@@ -1,0 +1,570 @@
+from concourse.mybir import dt, AluOpType, AxisListType, ActivationFunctionType
+
+OP = AluOpType
+AF = ActivationFunctionType
+F32, BF, I32, U16 = "float32", "bfloat16", "int32", "uint16"
+NDMA = 110
+SCRATCH = {
+    "XW0": ("sbuf", [128, 12304], BF), "XW1": ("sbuf", [128, 12304], BF),
+    "XB": ("sbuf", [128, 4096], BF), "W": ("sbuf", [128, 4096], BF), "KT": ("sbuf", [128, 4096], BF),
+    "WB": ("sbuf", [128, 16416], BF), "WF": ("sbuf", [128, 16384], F32),
+    "VT0": ("sbuf", [128, 4096], BF), "VT2": ("sbuf", [128, 4096], BF), "ST1": ("sbuf", [128, 4096], F32),
+    "ZB": ("sbuf", [128, 264], BF), "CR": ("sbuf", [128, 130], BF),
+    "IDF": ("sbuf", [128, 128], F32), "SHU": ("sbuf", [128, 128], F32),
+    "SHD": ("sbuf", [128, 128], F32), "TRI": ("sbuf", [128, 128], F32), "DF": ("sbuf", [128, 64], F32),
+    "MROW": ("sbuf", [128, 128], F32), "ONE": ("sbuf", [128, 2], F32), "PI": ("sbuf", [128, 8], I32),
+    "PC": ("sbuf", [128, 16], F32), "SEL": ("sbuf", [128, 128], BF), "G8": ("sbuf", [128, 16], F32),
+    "AT1": ("sbuf", [128, 256], F32), "ATK": ("sbuf", [128, 256], F32), "QT": ("sbuf", [128, 256], F32),
+    "EB": ("sbuf", [128, 258], F32), "SL0": ("sbuf", [128, 512], I32),
+    "NHB": ("sbuf", [128, 256], BF), "DHI": ("sbuf", [128, 256], BF), "DLO": ("sbuf", [128, 256], BF),
+    "HMB": ("sbuf", [128, 256], BF), "HM": ("sbuf", [128, 528], BF),
+    "BLB": ("sbuf", [128, 256], U16), "ELB": ("sbuf", [128, 256], U16), "BLW": ("sbuf", [128, 256], U16),
+    "VL": ("sbuf", [128, 256], U16), "QL0": ("sbuf", [128, 256], U16), "QL1": ("sbuf", [128, 256], U16),
+    "QL2": ("sbuf", [128, 256], U16),
+    "TA": ("sbuf", [128, 256], F32), "TB": ("sbuf", [128, 256], F32), "TC": ("sbuf", [128, 256], F32),
+    "TD": ("sbuf", [128, 256], F32), "TE": ("sbuf", [128, 256], F32),
+    "VI": ("sbuf", [128, 256], I32), "HI": ("sbuf", [128, 256], I32), "LI": ("sbuf", [128, 256], I32),
+    "S1": ("sbuf", [128, 256], BF), "S2": ("sbuf", [128, 256], BF), "FL": ("sbuf", [64, 528], BF),
+    "HB": ("sbuf", [128, 256], BF), "HB1": ("sbuf", [128, 256], BF),
+    "KEEP": ("sbuf", [128, 256], BF), "KEX": ("sbuf", [128, 256], F32), "R": ("sbuf", [128, 256], F32),
+    "INS": ("sbuf", [128, 256], BF), "KI": ("sbuf", [128, 256], BF), "IEX": ("sbuf", [128, 256], F32),
+    "IH": ("sbuf", [128, 256], F32), "TOP": ("sbuf", [128, 256], BF),
+    "PHI": ("sbuf", [128, 256], BF), "PLO": ("sbuf", [128, 256], BF),
+    "CROW": ("sbuf", [128, 128], F32), "TX": ("sbuf", [128, 256], BF),
+    "LX0": ("sbuf", [128, 256], BF), "LX1": ("sbuf", [128, 256], BF),
+    "ES0": ("sbuf", [128, 16], F32), "ES1": ("sbuf", [128, 16], F32),
+    "RE0": ("sbuf", [128, 16], F32), "RE1": ("sbuf", [128, 16], F32),
+}
+for _k in range(8):
+    SCRATCH["P%d" % _k] = ("psum", [128, 512], F32)
+SEMAPHORES = ["qv", "qs", "qt", "qg"] + ["d%d" % k for k in range(NDMA)]
+SEMAPHORES += ["%s%d" % (a, k) for a in ("xs", "xr", "es", "er") for k in range(2)]
+
+ALIAS = {"SC": (4096, 528, 64), "D1": (4640, 528, 64), "HIT": (5200, 256, 128), "KEY": (5456, 256, 128),
+         "Q0M": (5712, 256, 128)}
+S_P, S_M, S_A, S_D, S_N, S_B, S_0, S_01, S_K, S_I = 0, 8, 16, 24, 32, 40, 48, 56, 64, 72
+BIG = float(2 ** 24)
+KM, GB = 4112, 8208
+
+
+def rank_program(g, core, T, topo):
+    rank = T.rank_of(core)
+    if rank is None:
+        return
+    n = len(T.cores)
+    nxt, prv = T.cores[(rank + 1) % n], T.cores[(rank - 1) % n]
+    eng = {"v": g.vector, "s": g.scalar, "t": g.tensor, "g": g, "y": g.sync}
+    hist, known, cnt, total = {}, {q: {} for q in eng}, {q: 0 for q in eng}, {}
+    nd, serial = [0], [0]
+
+    def over(a, b):
+        if a[0] >= b[1] or b[0] >= a[1] or a[3] >= b[4] or b[3] >= a[4]:
+            return False
+        return not (a[2] == 16 and b[2] == 16 and a[0] % 16 != b[0] % 16)
+
+    def inside(a, b):
+        if not (b[0] <= a[0] and a[1] <= b[1] and b[3] <= a[3] and a[4] <= b[4]):
+            return False
+        return b[2] == 1 or (a[2] == 16 and a[0] % 16 == b[0] % 16)
+
+    def is_psum(name):
+        return name[0] == "P" and name[1:].isdigit()
+
+    def op(q, call, R, W, dma=False, remote=None):
+        deps = []
+        for name, reg in R:
+            ps = is_psum(name)
+            for r in hist.get(name, []):
+                if over(r["reg"], reg) and (r["w"] or (ps and r["q"] != q)):
+                    deps.append(r)
+        for name, reg in W:
+            for r in hist.get(name, []):
+                if over(r["reg"], reg) and not (q == "t" and r["q"] == "t"):
+                    deps.append(r)
+        deps.sort(key=lambda r: -r["n"])
+        kn = known[q]
+        for r in deps:
+            if kn.get(r["sem"], 0) >= r["val"]:
+                continue
+            eng[q].wait_ge(T.sem[r["sem"]], r["val"])
+            for k, v in r["vc"].items():
+                if kn.get(k, 0) < v:
+                    kn[k] = v
+            kn[r["sem"]] = r["val"]
+        ins = call()
+        serial[0] += 1
+        if remote is not None:
+            sem, val = remote
+        elif dma:
+            sem, val = "d%d" % nd[0], 16
+            nd[0] += 1
+            ins.then_inc(T.sem[sem], 16)
+        else:
+            cnt[q] += 1
+            sem, val = "q" + q, cnt[q]
+            ins.then_inc(T.sem[sem], 1)
+        total[sem] = val
+        vc = dict(kn)
+        for w, lst in ((False, R), (True, W)):
+            for name, reg in lst:
+                h = hist.setdefault(name, [])
+                if w or is_psum(name):
+                    h[:] = [r for r in h if not inside(r["reg"], reg)]
+                elif not dma and remote is None:
+                    h[:] = [r for r in h if r["w"] or r["dma"] or r["q"] != q or not inside(r["reg"], reg)]
+                h.append({"reg": reg, "w": w, "q": q, "sem": sem, "val": val, "vc": vc, "n": serial[0],
+                          "dma": dma or remote is not None})
+
+    def A(name, c0=0, c1=None, cs=1, p0=0, p1=None, ps=1):
+        if name in ALIAS:
+            o, k, r = ALIAS[name]
+            return A("WF", o + c0, o + (k if c1 is None else c1), cs, p0, r if p1 is None else p1, ps)
+        shape = T[name].shape
+        c1 = shape[1] if c1 is None else c1
+        p1 = shape[0] if p1 is None else p1
+        sc = slice(c0, c1) if cs == 1 else slice(c0, c1, cs)
+        sp = slice(p0, p1) if ps == 1 else slice(p0, p1, ps)
+        reg = (0, 128, 1, 0, 512) if is_psum(name) else (p0, p1, ps, c0, c1)
+        return T[name][sp, sc], [(name, reg)]
+
+    def IND(name, c0, c1, lst, l0, l1):
+        return (T[name][:, c0:c1].indirect(T[lst][:, l0:l1]),
+                [(name, (0, 128, 1, c0, c1)), (lst, (0, 128, 1, l0, l1))])
+
+    def outs(o):
+        return o[1][:1], o[1][1:]
+
+    def tt(o, a, b, f):
+        op("v", lambda: g.vector.tensor_tensor(o[0], a[0], b[0], f), a[1] + b[1], o[1])
+
+    def ts(o, a, s1, s2, f1, f2=None):
+        r = list(a[1])
+        x = [s1, s2]
+        for k in range(2):
+            if isinstance(x[k], tuple):
+                r += x[k][1]
+                x[k] = x[k][0]
+        if f2 is None:
+            op("v", lambda: g.vector.tensor_scalar(o[0], a[0], x[0], None, f1), r, o[1])
+        else:
+            op("v", lambda: g.vector.tensor_scalar(o[0], a[0], x[0], x[1], f1, f2), r, o[1])
+
+    def cp(o, a):
+        w, r = outs(o)
+        op("v", lambda: g.vector.tensor_copy(o[0], a[0]), a[1] + r, w)
+
+    def fill(o, val):
+        op("v", lambda: g.vector.memset(o[0], val), [], o[1])
+
+    def scan(o, a, b, f1, f2):
+        op("v", lambda: g.vector.tensor_tensor_scan(o[0], a[0], b[0], 0.0, f1, f2), a[1] + b[1], o[1])
+
+    def act(o, a, f=AF.Copy, bias=None):
+        w, r = outs(o)
+        if bias is None:
+            op("s", lambda: g.scalar.activation(o[0], a[0], f), a[1] + r, w)
+        else:
+            op("s", lambda: g.scalar.activation(o[0], a[0], f, bias=bias[0]), a[1] + r + bias[1], w)
+
+    def mm(o, l, r, start=True, stop=True):
+        op("t", lambda: g.tensor.matmul(o[0], l[0], r[0], start, stop), l[1] + r[1], o[1])
+
+    def dma(o, a, q="y"):
+        op(q, lambda: eng[q].dma_start(o[0], a[0]), a[1], o[1], dma=True)
+
+    def iota(o, pattern, base, mul, loose=True):
+        if loose:
+            op("g", lambda: g.iota(o[0], pattern, base, mul, allow_small_or_imprecise_dtypes=True), [], o[1])
+        else:
+            op("g", lambda: g.iota(o[0], pattern, base, mul), [], o[1])
+
+    def IO(name, *idx):
+        return (T[name][idx] if idx else T[name][:]), []
+
+    def sel(c, k=8):
+        return A("SEL", c, c + k)
+
+    def tr(o, a):
+        mm(o, a, A("IDF"))
+
+    def rows(name, off, r, src, q="y"):
+        dma(A(name, off, off + 4096, 1, r, 128, 16), src, q)
+
+    dma(A("VI"), IO("ends"), "y")
+    dma(A("SL0"), IO("start"), "s")
+    fill(A("XW0", 0, 16), 0.0)
+    fill(A("XW0", 4104, 4112), 0.0)
+    dma(A("XW0", 15, 4111), IO("x"), "y")
+    dma(A("W"), IO("w"), "s")
+
+    iota(A("PI", 0, 1), [[0, 1]], 0, 1, False)
+    iota(A("TA"), [[1, 256]], 0, 0)
+    iota(A("TB"), [[0, 2], [1, 128]], 0, 0)
+    iota(A("TC"), [[128, 2], [0, 128]], 0, 0)
+    iota(A("TE", 0, 128), [[-1, 128]], 0, 1)
+    iota(A("G8", 0, 8), [[-16, 8]], 0, 1)
+    iota(A("TRI"), [[1, 8], [0, 16]], 0, 0)
+    iota(A("CR", 0, 64), [[1, 64]], -64, 0)
+    iota(A("CR", 64, 130), [[1, 66]], 0, 0)
+    iota(A("QT"), [[128, 2], [0, 8], [256, 16]], 0, 1)
+    iota(A("MROW", 0, 128), [[0, 8], [1, 16]], 0, 0)
+    iota(A("KEX"), [[0, 16], [256, 16]], 0, 0)
+    iota(A("IEX"), [[1, 16], [0, 16]], 0, 0)
+    fill(A("KT"), 0.0)
+    pi = lambda k: A("PI", k, k + 1)
+    pc = lambda k: A("PC", k, k + 1)
+    ts(pi(1), pi(0), 15, None, OP.bitwise_and)
+    ts(pi(2), pi(0), 4, None, OP.arith_shift_right)
+    ts(pi(3), pi(0), 7, None, OP.bitwise_and)
+    cp(pc(0), pi(1))
+    ts(pc(1), pc(0), 256.0, None, OP.mult)
+    ts(A("AT1"), A("TA"), pc(1), 1.0, OP.add, OP.add)
+    cp(A("PLO"), A("TB"))
+    ts(A("PHI"), A("TC"), pc(1), None, OP.add)
+    rows("KT", 0, 0, A("PLO"), "y")
+    rows("KT", 0, 1, A("PHI"), "s")
+    cp(pc(2), pi(2))
+    ts(A("IDF"), A("TE", 0, 128), 0.0, None, OP.is_equal)
+    ts(A("SHU"), A("TE", 0, 128), 1.0, None, OP.is_equal)
+    ts(pc(5), pc(0), 15.0, 8192.0, OP.is_equal, OP.mult)
+    ts(A("G8", 8, 16), A("G8", 0, 8), 0.0, None, OP.is_ge)
+    ts(A("G8", 0, 8), A("G8", 0, 8), 15.0, None, OP.is_le)
+    tt(A("G8", 0, 8), A("G8", 0, 8), A("G8", 8, 16), OP.mult)
+
+    def selector(c, lo, hi, v=1.0):
+        ts(pc(8), pc(0), float(lo), None, OP.is_ge)
+        ts(pc(9), pc(0), float(hi), v, OP.is_le, OP.mult)
+        ts(sel(c), A("G8", 0, 8), pc(8), pc(9), OP.mult, OP.mult)
+    selector(S_P, 0, 15)
+    selector(S_M, 0, 15, -1.0)
+    selector(S_A, 0, 2)
+    selector(S_D, 3, 4)
+    selector(S_N, 2, 2)
+    selector(S_01, 0, 1)
+    tt(sel(S_B), sel(S_01), sel(S_D), OP.add)
+    fill(A("ZB"), 0.0)
+
+    def late_constants():
+        selector(S_0, 0, 0)
+        selector(S_K, 0, 1)
+        selector(S_I, 2, 3)
+        fill(pc(10), -1.0)
+        fill(pc(11), -2.0)
+        ts(pc(6), pc(0), 14.0, None, OP.is_le)
+        ts(A("SHD"), A("TE", 0, 128), -1.0, pc(6), OP.is_equal, OP.mult)
+        ts(A("TRI"), A("TRI"), pc(2), None, OP.is_equal)
+        ts(A("TE", 128, 256), A("TE", 0, 128), 0.0, None, OP.is_lt)
+        tt(A("TRI"), A("TRI"), A("TE", 128, 256), OP.mult)
+        tt(A("DF"), A("SHU", 0, 64), A("IDF", 0, 64), OP.subtract)
+        ts(A("TE", 128, 192), A("TE", 0, 64), -1.0, None, OP.is_equal)
+        tt(A("DF"), A("DF"), A("IDF", 0, 64), OP.subtract)
+        tt(A("DF"), A("DF"), A("TE", 128, 192), OP.add)
+        fill(A("DF", 0, 1, 1, 0, 1), -1.0)
+        ts(A("MROW", 0, 128), A("MROW", 0, 128), 1.0, None, OP.min)
+        fill(A("ONE"), 1.0)
+        ts(A("ATK"), A("AT1"), -1.0, 1.0, OP.add, OP.max)
+        ts(A("ATK"), A("ATK"), 4096.0, None, OP.mult)
+        fill(A("HM"), 0.0)
+        fill(A("WB", 16384, 16416), 0.0)
+        cp(pc(3), pi(3))
+        ts(pc(4), pc(3), 16.0, None, OP.mult)
+        tt(pc(7), pc(0), pc(3), OP.subtract)
+        ts(pc(7), pc(7), 16.0, None, OP.mult)
+        for name in ("VT0", "ST1", "VT2"):
+            iota(A(name), [[0, 4096]], 0, 0)
+        for name, la, ha, lt, ht in (("VT0", 0, 0, "PLO", "PHI"), ("ST1", 65, 4032, "R", "IH"),
+                                     ("VT2", 1, 8192, "HB", "HB1")):
+            ts(A(lt), A("IEX"), pc(4), float(la), OP.add, OP.add)
+            ts(A(ht), A("KEX"), pc(7), float(ha), OP.add, OP.add)
+            rows(name, 0, 0, A(lt))
+            rows(name, 0, 1, A(ht))
+
+    zb = lambda k: A("ZB", 0, k)
+    half = lambda nm, h: A(nm, 128 * h, 128 * h + 128)
+
+    def exts(buf, off, h, out, s, k=8, start=True, stop=True):
+        for i in range(16):
+            mm(A(out, i, i + (k - 1) * 16 + 1, 16), A(buf, off + 2048 * h + i, off + 2048 * h + 2048, 16), sel(s, k),
+               start, stop if stop is True else (stop == "last" and i == 15))
+
+    def maxcarry(col):
+        mm(A("P4", 0, 128, 1, 0, 1), col, A("SHD"))
+        scan(A("CROW", 0, 128, 1, 0, 1), A("MROW", 0, 128, 1, 0, 1), A("P4", 0, 128, 1, 0, 1), OP.mult, OP.max)
+        mm(A("P5", 0, 1), A("CROW", 0, 128, 1, 0, 1), A("ONE", 0, 1, 1, 0, 1))
+        return A("P5", 0, 1)
+
+    def sumcarry(col):
+        mm(A("P5", 8, 9), A("TRI"), col)
+        return A("P5", 8, 9)
+
+    def split(hi, lo, src):
+        cp(hi, src)
+        tt(lo, src, hi, OP.subtract)
+
+    for t in range(2):
+        X, XO = "XW%d" % t, "XW%d" % (1 - t)
+        if t == 0:
+            cp(A("EB", 0, 256), A("VI"))
+        mm(A("P4", 0, 1), A("SHU"), A("EB", 0, 1))
+        tt(A("NHB"), A("EB", 0, 256), A("AT1"), OP.is_gt)
+        rows("KT", 0, 2, A("NHB"), "y")
+        ts(A("EB", 256, 257), A("P4", 0, 1), pc(5), None, OP.add)
+        tt(A("TC"), A("EB", 1, 257), A("EB", 0, 256), OP.is_lt)
+        tt(A("TD"), A("EB", 1, 257), A("AT1"), OP.subtract)
+        tt(A("TD"), A("TD"), A("TC"), OP.mult)
+        cp(A("DHI"), A("TD"))
+        rows("KT", 0, 3, A("DHI"), "s")
+        tt(A("DLO"), A("TD"), A("DHI"), OP.subtract)
+        rows("KT", 0, 4, A("DLO"), "y")
+        for h in range(2):
+            cp(half("VL", h), A("SL0", 256 * t + 128 * h, 256 * t + 128 * h + 128))
+        tt(A("TC"), A("TD"), A("AT1"), OP.add)
+        ts(A("BLB"), A("TC"), 15.0, None, OP.add)
+        ts(A("ELB"), A("EB", 0, 256), -1.0, None, OP.add)
+        if t == 0:
+            late_constants()
+
+        def xa(h):
+            tt(A("WB", 4096 + 2048 * h, 6144 + 2048 * h), IND(X, 16, 4112, "VL", 128 * h, 128 * h + 128),
+               A("W", 2048 * h, 2048 * h + 2048), OP.min)
+            mm(A("P%d" % h, 0, 128), zb(128), zb(128), True, False)
+            exts("WB", 4096, h, "P%d" % h, S_P, 8, False, False)
+
+        def xb(h):
+            tt(A("WB", 8192 + 2048 * h, 10240 + 2048 * h), IND("XB", 0, 4096, "VL", 128 * h, 128 * h + 128),
+               A("W", 2048 * h, 2048 * h + 2048), OP.min)
+            exts("WB", 8192, h, "P%d" % h, S_M, 8, False, "last")
+
+        def kid(h):
+            act(A("WB", 12288 + 2048 * h, 14336 + 2048 * h), IND("KT", 0, 4096, "VL", 128 * h, 128 * h + 128))
+            exts("WB", 12288, h, "P%d" % (2 + h), S_A, 24)
+
+        def small(h, last):
+            ts(half("TA", h), A("P%d" % h, 0, 128), 0.0, None, OP.is_gt)
+            tt(half("TB", h), A("P%d" % (2 + h), 128, 256), half("TA", h), OP.mult)
+            tt(half("VI" if last else "TC", h), A("P%d" % (2 + h), 0, 128), half("TB", h), OP.add)
+            if not last:
+                tr(A("P%d" % (4 + h), 0, 128), half("TC", h))
+
+        def relist(h):
+            cp(half("VL", h), A("P%d" % (4 + h), 0, 128))
+
+        for s in range(4):
+            xa(0)
+            if s == 0:
+                for h in range(2):
+                    exts("KT", 0, h, "P%d" % (4 + h), S_B)
+                for h in range(2):
+                    ts(half("TD", h), A("P%d" % (4 + h), 0, 128), 16.0, None, OP.add)
+                    tr(A("P%d" % (6 + h), 0, 128), half("TD", h))
+                for h in (1, 0):
+                    cp(half("BLW", h), A("P%d" % (6 + h), 0, 128))
+                act(A("XB", 2048, 4096), IND(X, 0, 4112, "BLW", 128, 256))
+                cp(A("XB", 0, 2048), IND(X, 0, 4112, "BLW", 0, 128))
+                kid(0)
+            else:
+                kid(0)
+                small(1, False)
+            xb(0)
+            if s > 0:
+                relist(1)
+            xa(1)
+            kid(1)
+            if s == 0:
+                ts(A("KEY"), A("EB", 0, 256), 4096.0, None, OP.mult)
+                tt(A("KEY"), A("KEY"), A("AT1"), OP.subtract)
+                tt(A("KEY"), A("KEY"), A("NHB"), OP.mult)
+                ts(A("HMB"), A("NHB"), -BIG, BIG, OP.mult, OP.add)
+                for q in range(8):
+                    dma(A("HM", 66 * q, 66 * q + 64, 1, 0, 64), A("HMB", 0, 256, 1, 16 * q, 16 * q + 16))
+                iota(A("WB", 0, 4096), [[0, 4096]], 0, 0)
+                iota(A("WF", 0, 4096), [[0, 4096]], 0, 0)
+            if s == 1:
+                act(half("HIT", 0), A("P2", 256, 384))
+                act(half("HIT", 1), A("P3", 256, 384))
+            small(0, s == 3)
+            xb(1)
+            if s < 3:
+                relist(0)
+            if s in (1, 2):
+                o = 4112 if s == 1 else 8208
+                act(A(X, o, o + 4096), A(X, 15, 4111), AF.Relu, pc(9 + s))
+
+        mm(A("P6", 0, 264, 1, 0, 64), zb(64), zb(264), True, False)
+        mm(A("P7", 0, 264, 1, 0, 64), zb(64), zb(264), True, False)
+        slot = 0
+        for h in range(2):
+            if h == 1:
+                small(1, True)
+            ts(half("HI", h), half("VI", h), 6, None, OP.arith_shift_right)
+            ts(half("LI", h), half("VI", h), 63, None, OP.bitwise_and)
+            ts(half("TA", h), half("HI", h), -64.0, None, OP.add)
+            ts(half("S2", h), half("LI", h), 1.0, None, OP.add)
+            tt(half("S1", h), half("TA", h), half("HIT", h), OP.mult)
+            for q in range(8):
+                for i in range(16):
+                    c = 128 * h + 16 * q + i
+                    o = 130 * (slot % 94)
+                    slot += 1
+                    ts(A(XO, o, o + 130), A("CR"), A("S1", c, c + 1), A("S2", c, c + 1), OP.max, OP.min)
+                    mm(A("P%d" % (6 + q // 4), 66 * (q % 4), 66 * (q % 4) + 66, 1, 0, 64), A(XO, o, o + 64),
+                       A(XO, o + 64, o + 130), False, h == 1 and i == 15 and q % 4 == 3)
+        act(A("SC", 0, 264), A("P6", 0, 264, 1, 0, 64))
+        cp(A("SC", 264, 528), A("P7", 0, 264, 1, 0, 64))
+        tt(A("D1", 0, 527), A("SC", 1, 528), A("SC", 0, 527), OP.subtract)
+        tt(A("SC", 0, 526), A("D1", 0, 526), A("D1", 1, 527), OP.subtract)
+        for b, (c0, c1) in enumerate(((0, 264), (264, 526))):
+            mm(A("P%d" % (6 + b), 0, c1 - c0, 1, 0, 64), A("DF", 0, 64, 1, 0, 64), A("SC", c0, c1))
+            tt(A("FL", c0, c1), A("P%d" % (6 + b), 0, c1 - c0, 1, 0, 64), A("HM", c0, c1, 1, 0, 64), OP.mult)
+        for q in range(8):
+            dma(A(XO, 15, 4111, 1, 16 * q, 16 * q + 1), A("FL", 66 * q, 66 * q + 64), "y" if q % 2 else "s")
+        dma(A("HB"), A(XO, 15, 4111, 1, 0, 128, 16), "y")
+        dma(A("HB1"), A(XO, 16, 4112, 1, 0, 128, 16), "y")
+
+        act(A(XO, GB, GB + 2048), IND(XO, 0, 4112, "BLB", 0, 128))
+        cp(A(XO, GB + 2048, GB + 4096), IND(XO, 0, 4112, "BLB", 128, 256))
+        for h in range(2):
+            exts(XO, GB, h, "P%d" % h, S_0)
+        ts(A("KEEP"), A("HB"), 0.0, None, OP.is_le)
+        fill(A("TE"), 0.0)
+        scan(A("TA"), A("KEEP"), A("TE"), OP.add, OP.add)
+        k0 = sumcarry(A("TA", 255, 256))
+        for h in range(2):
+            ts(half("TB", h), A("P%d" % h, 0, 128), 0.0, BIG, OP.is_gt, OP.mult)
+            tr(A("P2", 128 * h, 128 * h + 128), half("TB", h))
+        ts(A("TA"), A("TA"), k0, None, OP.add)
+        split(A("PHI"), A("PLO"), A("TA"))
+        rows(XO, KM, 0, A("PHI"), "y")
+        rows(XO, KM, 1, A("PLO"), "y")
+        tt(A("KEX"), A("TA"), A("KEEP"), OP.subtract)
+        tt(A("TC"), A("P2", 0, 256), A("HB1"), OP.add)
+        tt(A("TC"), A("TC"), A("KEY"), OP.min)
+        scan(A("R"), A("TC"), A("TC"), OP.max, OP.max)
+        c = maxcarry(A("R", 255, 256))
+        ts(A("R"), A("R"), c, None, OP.max)
+        tt(A("INS"), A("R"), A("ATK"), OP.is_ge)
+        tt(A("KI"), A("KEEP"), A("INS"), OP.mult)
+        scan(A("TA"), A("KI"), A("TE"), OP.add, OP.add)
+        c = sumcarry(A("TA", 255, 256))
+        tt(A("TOP"), A("R"), A("TC"), OP.is_equal)
+        tt(A("TOP"), A("TOP"), A("INS"), OP.mult)
+        ts(A("TA"), A("TA"), c, None, OP.add)
+        split(A("DHI"), A("DLO"), A("TA"))
+        rows(XO, KM, 2, A("DHI"), "y")
+        rows(XO, KM, 3, A("DLO"), "y")
+        for h in range(2):
+            act(A(XO, GB + 2048 * h, GB + 2048 * h + 2048), IND(XO, KM, KM + 4096, "ELB", 128 * h, 128 * h + 128))
+            exts(XO, GB, h, "P%d" % h, S_K, 16)
+        tt(A("IEX"), A("TA"), A("KI"), OP.subtract)
+        tt(A("TB"), A("TOP"), A("IEX"), OP.mult)
+        scan(A("IH"), A("TB"), A("TB"), OP.max, OP.max)
+        c = maxcarry(A("IH", 255, 256))
+        ts(A("IH"), A("IH"), c, None, OP.max)
+        tt(A("TB"), A("IH"), A("IEX"), OP.subtract)
+        tt(A("TB"), A("TB"), A("INS"), OP.mult)
+        tt(A("TB"), A("TB"), A("IEX"), OP.add)
+        ts(A("TB"), A("TB"), 2.0, None, OP.mult)
+        tt(A("TB"), A("TB"), A("KEX"), OP.add)
+        ts(A("TD"), A("AT1"), 12287.0, None, OP.add)
+        tt(A("TB"), A("TB"), A("TD"), OP.subtract)
+        tt(A("TC"), A("TB"), A("KEEP"), OP.mult)
+        tt(A("TC"), A("TC"), A("TD"), OP.add)
+        cp(A("QL0"), A("TC"))
+        sc0 = lambda k: cp(IND("WB", 0, 16384, "QL0", 64 * k, 64 * k + 64), A("VT0", 1024 * k, 1024 * k + 1024))
+        sc2 = lambda k: cp(IND("WB", 0, 16384, "QL2", 64 * k, 64 * k + 64), A("VT2", 1024 * k, 1024 * k + 1024))
+        sc0(0)
+        tt(A("TB"), A("TB"), A("KI"), OP.mult)
+        tt(A("Q0M"), A("TB"), A("TD"), OP.add)
+        ts(A("TE"), A("INS"), -2.0, 2.0, OP.mult, OP.add)
+        sc0(1)
+        for h in range(2):
+            cp(half("TA", h), A("P%d" % h, 128, 256))
+            tr(A("P2", 128 * h, 128 * h + 128), half("TA", h))
+        for h in range(2):
+            cp(half("TB", h), A("P%d" % h, 0, 128))
+            tr(A("P3", 128 * h, 128 * h + 128), half("TB", h))
+        tt(A("TC"), A("P2", 0, 256), A("TOP"), OP.mult)
+        scan(A("R"), A("TC"), A("TC"), OP.max, OP.max)
+        c = maxcarry(A("R", 255, 256))
+        tt(A("TD"), A("P2", 0, 256), A("IEX"), OP.subtract)
+        tt(A("TD"), A("TD"), A("TE"), OP.mult)
+        ts(A("R"), A("R"), c, None, OP.max)
+        tt(A("R"), A("R"), A("IH"), OP.subtract)
+        tt(A("R"), A("R"), A("KI"), OP.mult)
+        tt(A("TC"), A("Q0M"), A("R"), OP.add)
+        cp(A("QL1"), A("TC"))
+        for k in range(4):
+            act(IND("WF", 0, 16384, "QL1", 64 * k, 64 * k + 64), A("ST1", 1024 * k, 1024 * k + 1024), AF.Silu)
+        tt(A("TC"), A("TC"), A("R"), OP.add)
+        cp(A("QL2"), A("TC"))
+        tt(A("TA"), A("P3", 0, 256), A("KEX"), OP.subtract)
+        tt(A("TA"), A("TA"), A("TD"), OP.add)
+        split(A("PHI"), A("PLO"), A("TA"))
+        sc0(2)
+        sc0(3)
+        for k in range(4):
+            sc2(k)
+        for k in range(3):
+            o = 4096 + (15, 4112, 8208)[k]
+            rows("WB", o, 0, A("PHI"), "y")
+            rows("WB", o, 1, A("PLO"), "y")
+        act(A("XB", 2048, 4096), A("WF", 2048, 4096))
+        act(A("XB", 0, 2048), A("WF", 0, 2048))
+        for h in (1, 0):
+            mm(A("P%d" % h, 0, 128), zb(128), zb(128), True, False)
+            exts("WB", 0, h, "P%d" % h, S_01, 8, False, False)
+            exts("XB", 0, h, "P%d" % h, S_01, 8, False, "last")
+            ts(half("TB", h), A("P%d" % h, 0, 128), 15.0, None, OP.add)
+            tr(A("P%d" % (2 + h), 0, 128), half("TB", h))
+            cp(half("VL", h), A("P%d" % (2 + h), 0, 128))
+        LX, ES, RE = ["%s%d" % (nm, t) for nm in ("LX", "ES", "RE")]
+        dx = 15 if t == 0 else 0
+        SZ = lambda a, b: IND("WB", 4096, 16400, "VL", a, b)
+        XI = lambda a, b: IND(X, 0, 12304, "VL", a, b)
+        cp(A("TX"), XI(240, 256))
+        act(A(XO, GB + 3840, GB + 4096), SZ(240, 256))
+        for h in range(2):
+            mm(A("P4", 8 * h, 8 * h + 8), A(XO, GB + 3840 + 128 * h, GB + 3968 + 128 * h), sel(S_01))
+        tt(A(ES), A("P4", 0, 16), A("QT", 15, 256, 16), OP.add)
+        ts(A(ES), A(ES), 4096.0, None, OP.min)
+        rid, pid, _se = topo.addr(nxt)
+        m = topo.mask(core, nxt)
+        ne, nb = len(topo.engines(core, nxt)), len(topo.engines(prv, core))
+
+        def send(src, dst, ss, rs):
+            sa, da = A(src), T[dst][:]
+            op("g", lambda: g.remote_dma(da, sa[0], T.sem[rs], T.sem[ss], pid, rid, m), sa[1], [], remote=(ss, ne))
+            total[rs] = nb
+            hist[dst] = [{"reg": (0, 128, 1, 0, 256), "w": True, "q": "remote", "sem": rs, "val": nb, "vc": {}, "n": 0,
+                          "dma": True}]
+        send("TX", LX, "xs%d" % t, "xr%d" % t)
+        send(ES, RE, "es%d" % t, "er%d" % t)
+        cp(A(XO, dx + 2048, dx + 3840), XI(128, 240))
+        act(A(XO, GB + 2048, GB + 3840), SZ(128, 240))
+        if t == 1:
+            dma(IO("y", slice(0, 128), slice(2048, 3840)), A(XO, dx + 2048, dx + 3840))
+        cp(A(XO, dx, dx + 2048), XI(0, 128))
+        act(A(XO, GB, GB + 2048), SZ(0, 128))
+        for i in list(range(8, 15)) + list(range(8)):
+            for h in range(2):
+                mm(A("P5", 128 * h + i, 128 * h + 113 + i, 16),
+                   A(XO, GB + 256 * i + 128 * h, GB + 256 * i + 128 * h + 128), sel(S_01))
+        for h in range(2):
+            mm(A("P5", 128 * h + 15, 128 * h + 128, 16), zb(128), zb(8))
+        if t == 0:
+            cp(A(XO, 3855, 4111), A(LX))
+        else:
+            dma(IO("y", slice(0, 128), slice(0, 2048)), A(XO, dx, dx + 2048))
+            dma(IO("y", slice(0, 128), slice(3840, 4096)), A(LX))
+        tt(A("TA"), A("P5", 0, 256), A("QT"), OP.add)
+        ts(A("TA"), A("TA"), 3840.0, None, OP.min)
+        cp(A("TA", 15, 256, 16), A(RE))
+        for h in range(2):
+            tr(A("P6", 128 * h, 128 * h + 128), half("TA", h))
+        cp(A("EB", 0, 256), A("P6", 0, 256))
+        if t == 1:
+            dma(IO("ye"), A("EB", 0, 256))
+
+    for s in sorted(total):
+        if known["g"].get(s, 0) < total[s]:
+            g.wait_ge(T.sem[s], total[s])

@@ -9,13 +9,14 @@ SCRATCH = {
     "XB": ("sbuf", [128, 4096], BF), "W": ("sbuf", [128, 4096], BF), "KT": ("sbuf", [128, 4096], BF),
     "WB": ("sbuf", [128, 16416], BF), "WF": ("sbuf", [128, 16384], F32),
     "VT0": ("sbuf", [128, 4096], BF), "VT2": ("sbuf", [128, 4096], BF), "ST1": ("sbuf", [128, 4096], F32),
-    "ZB": ("sbuf", [128, 264], BF), "CR": ("sbuf", [128, 130], BF),
+    "ST2": ("sbuf", [128, 1024], F32),
+    "ZB": ("sbuf", [128, 264], BF), "CR": ("sbuf", [128, 132], BF),
     "IDF": ("sbuf", [128, 128], F32), "SHU": ("sbuf", [128, 128], F32),
     "SHD": ("sbuf", [128, 128], F32), "TRI": ("sbuf", [128, 128], F32), "DF": ("sbuf", [128, 64], F32),
     "MROW": ("sbuf", [128, 128], F32), "ONE": ("sbuf", [128, 2], F32), "PI": ("sbuf", [128, 8], I32),
-    "PC": ("sbuf", [128, 16], F32), "SEL": ("sbuf", [128, 128], BF), "G8": ("sbuf", [128, 16], F32),
+    "PC": ("sbuf", [128, 16], F32), "SEL": ("sbuf", [128, 128], BF),
     "AT1": ("sbuf", [128, 256], F32), "ATK": ("sbuf", [128, 256], F32), "QT": ("sbuf", [128, 256], F32),
-    "EB": ("sbuf", [128, 258], F32), "SL0": ("sbuf", [128, 512], I32),
+    "EB": ("sbuf", [128, 258], F32),
     "NHB": ("sbuf", [128, 256], BF), "DHI": ("sbuf", [128, 256], BF), "DLO": ("sbuf", [128, 256], BF),
     "HMB": ("sbuf", [128, 256], BF), "HM": ("sbuf", [128, 528], BF),
     "BLB": ("sbuf", [128, 256], U16), "ELB": ("sbuf", [128, 256], U16), "BLW": ("sbuf", [128, 256], U16),
@@ -23,7 +24,7 @@ SCRATCH = {
     "QL2": ("sbuf", [128, 256], U16),
     "TA": ("sbuf", [128, 256], F32), "TB": ("sbuf", [128, 256], F32), "TC": ("sbuf", [128, 256], F32),
     "TD": ("sbuf", [128, 256], F32), "TE": ("sbuf", [128, 256], F32),
-    "VI": ("sbuf", [128, 256], I32), "HI": ("sbuf", [128, 256], I32), "LI": ("sbuf", [128, 256], I32),
+    "VI": ("sbuf", [128, 256], I32), "HI": ("sbuf", [128, 256], I32),
     "S1": ("sbuf", [128, 256], BF), "S2": ("sbuf", [128, 256], BF), "FL": ("sbuf", [64, 528], BF),
     "HB": ("sbuf", [128, 256], BF), "HB1": ("sbuf", [128, 256], BF),
     "KEEP": ("sbuf", [128, 256], BF), "KEX": ("sbuf", [128, 256], F32), "R": ("sbuf", [128, 256], F32),
@@ -40,7 +41,7 @@ for _k in range(8):
 SEMAPHORES = ["qv", "qs", "qt", "qg"] + ["d%d" % k for k in range(NDMA)]
 SEMAPHORES += ["%s%d" % (a, k) for a in ("xs", "xr", "es", "er") for k in range(2)]
 
-ALIAS = {"SC": (4096, 528, 64), "D1": (4640, 528, 64), "HIT": (5200, 256, 128), "KEY": (5456, 256, 128),
+ALIAS = {"SC": (4096, 528, 65), "D1": (4640, 528, 65), "HIT": (5200, 256, 128), "KEY": (5456, 256, 128),
          "Q0M": (5712, 256, 128)}
 S_P, S_M, S_A, S_D, S_N, S_B, S_0, S_01, S_K, S_I = 0, 8, 16, 24, 32, 40, 48, 56, 64, 72
 BIG = float(2 ** 24)
@@ -159,12 +160,12 @@ def rank_program(g, core, T, topo):
     def scan(o, a, b, f1, f2):
         op("v", lambda: g.vector.tensor_tensor_scan(o[0], a[0], b[0], 0.0, f1, f2), a[1] + b[1], o[1])
 
-    def act(o, a, f=AF.Copy, bias=None):
+    def act(o, a, f=AF.Copy, bias=None, scale=1.0):
         w, r = outs(o)
         if bias is None:
             op("s", lambda: g.scalar.activation(o[0], a[0], f), a[1] + r, w)
         else:
-            op("s", lambda: g.scalar.activation(o[0], a[0], f, bias=bias[0]), a[1] + r + bias[1], w)
+            op("s", lambda: g.scalar.activation(o[0], a[0], f, bias=bias[0], scale=scale), a[1] + r + bias[1], w)
 
     def mm(o, l, r, start=True, stop=True):
         op("t", lambda: g.tensor.matmul(o[0], l[0], r[0], start, stop), l[1] + r[1], o[1])
@@ -191,30 +192,47 @@ def rank_program(g, core, T, topo):
         dma(A(name, off, off + 4096, 1, r, 128, 16), src, q)
 
     dma(A("VI"), IO("ends"), "y")
-    dma(A("SL0"), IO("start"), "s")
+    dma(A("HI"), IO("start", slice(0, 128), slice(0, 256)), "s")
     fill(A("XW0", 0, 16), 0.0)
     fill(A("XW0", 4104, 4112), 0.0)
     dma(A("XW0", 15, 4111), IO("x"), "y")
     dma(A("W"), IO("w"), "s")
 
+    def pick(o, pattern, f, v, base, mul):
+        op("g", lambda: g.affine_select(o[0], o[0], pattern, f, v, base, mul), o[1], o[1])
+
+    def selector(c, lo, hi):
+        pick(sel(c), [[-16, 8]], OP.is_ge, 0.0, -lo, 1)
+        pick(sel(c), [[16, 8]], OP.is_ge, 0.0, hi, -1)
+
+    def one_group(nm):
+        pick(A(nm), [[-16, 8], [0, 16]], OP.is_ge, 0.0, 0, 1)
+        pick(A(nm), [[16, 8], [0, 16]], OP.is_ge, 0.0, 15, -1)
+
+    for nm, v in (("SHU", 0.0), ("SEL", 1.0), ("IDF", 0.0), ("SHD", 0.0), ("TRI", 1.0), ("DF", 0.0)):
+        fill(A(nm), v)
+    fill(sel(S_M), -1.0)
+    fill(A("ZB"), 0.0)
+    fill(A("ONE"), 1.0)
+    fill(A("KT"), 0.0)
     iota(A("PI", 0, 1), [[0, 1]], 0, 1, False)
     iota(A("TA"), [[1, 256]], 0, 0)
     iota(A("TB"), [[0, 2], [1, 128]], 0, 0)
     iota(A("TC"), [[128, 2], [0, 128]], 0, 0)
-    iota(A("TE", 0, 128), [[-1, 128]], 0, 1)
-    iota(A("G8", 0, 8), [[-16, 8]], 0, 1)
-    iota(A("TRI"), [[1, 8], [0, 16]], 0, 0)
-    iota(A("CR", 0, 64), [[1, 64]], -64, 0)
-    iota(A("CR", 64, 130), [[1, 66]], 0, 0)
+    pick(A("SHU"), [[-1, 128]], OP.not_equal, 1.0, -1, 1)
+    for c, lo, hi in ((S_B, 0, 4), (S_P, 0, 15), (S_M, 0, 15), (S_A, 0, 2), (S_D, 3, 4), (S_N, 2, 2)):
+        selector(c, lo, hi)
+    pick(sel(S_B), [[-16, 8]], OP.not_equal, 0.0, -2, 1)
+    pick(A("IDF"), [[-1, 128]], OP.not_equal, 1.0, 0, 1)
+    iota(A("CR", 0, 65), [[1, 65]], -65, 0)
+    iota(A("CR", 65, 131), [[1, 66]], 0, 0)
     iota(A("QT"), [[128, 2], [0, 8], [256, 16]], 0, 1)
     iota(A("MROW", 0, 128), [[0, 8], [1, 16]], 0, 0)
     iota(A("KEX"), [[0, 16], [256, 16]], 0, 0)
     iota(A("IEX"), [[1, 16], [0, 16]], 0, 0)
-    fill(A("KT"), 0.0)
     pi = lambda k: A("PI", k, k + 1)
     pc = lambda k: A("PC", k, k + 1)
     ts(pi(1), pi(0), 15, None, OP.bitwise_and)
-    ts(pi(2), pi(0), 4, None, OP.arith_shift_right)
     ts(pi(3), pi(0), 7, None, OP.bitwise_and)
     cp(pc(0), pi(1))
     ts(pc(1), pc(0), 256.0, None, OP.mult)
@@ -223,45 +241,20 @@ def rank_program(g, core, T, topo):
     ts(A("PHI"), A("TC"), pc(1), None, OP.add)
     rows("KT", 0, 0, A("PLO"), "y")
     rows("KT", 0, 1, A("PHI"), "s")
-    cp(pc(2), pi(2))
-    ts(A("IDF"), A("TE", 0, 128), 0.0, None, OP.is_equal)
-    ts(A("SHU"), A("TE", 0, 128), 1.0, None, OP.is_equal)
     ts(pc(5), pc(0), 15.0, 8192.0, OP.is_equal, OP.mult)
-    ts(A("G8", 8, 16), A("G8", 0, 8), 0.0, None, OP.is_ge)
-    ts(A("G8", 0, 8), A("G8", 0, 8), 15.0, None, OP.is_le)
-    tt(A("G8", 0, 8), A("G8", 0, 8), A("G8", 8, 16), OP.mult)
-
-    def selector(c, lo, hi, v=1.0):
-        ts(pc(8), pc(0), float(lo), None, OP.is_ge)
-        ts(pc(9), pc(0), float(hi), v, OP.is_le, OP.mult)
-        ts(sel(c), A("G8", 0, 8), pc(8), pc(9), OP.mult, OP.mult)
-    selector(S_P, 0, 15)
-    selector(S_M, 0, 15, -1.0)
-    selector(S_A, 0, 2)
-    selector(S_D, 3, 4)
-    selector(S_N, 2, 2)
-    selector(S_01, 0, 1)
-    tt(sel(S_B), sel(S_01), sel(S_D), OP.add)
-    fill(A("ZB"), 0.0)
 
     def late_constants():
-        selector(S_0, 0, 0)
-        selector(S_K, 0, 1)
-        selector(S_I, 2, 3)
+        for c, lo, hi in ((S_0, 0, 0), (S_01, 0, 1), (S_K, 0, 1), (S_I, 2, 3)):
+            selector(c, lo, hi)
+        pick(A("SHD"), [[-1, 128]], OP.not_equal, 1.0, 1, 1)
+        one_group("SHD")
+        pick(A("TRI"), [[1, 128]], OP.is_ge, 0.0, -1, -1)
+        one_group("TRI")
+        for k, v in ((0, 1.0), (1, -2.0), (2, 1.0)):
+            pick(A("DF"), [[-1, 64]], OP.not_equal, v, -k, 1)
         fill(pc(10), -1.0)
         fill(pc(11), -2.0)
-        ts(pc(6), pc(0), 14.0, None, OP.is_le)
-        ts(A("SHD"), A("TE", 0, 128), -1.0, pc(6), OP.is_equal, OP.mult)
-        ts(A("TRI"), A("TRI"), pc(2), None, OP.is_equal)
-        ts(A("TE", 128, 256), A("TE", 0, 128), 0.0, None, OP.is_lt)
-        tt(A("TRI"), A("TRI"), A("TE", 128, 256), OP.mult)
-        tt(A("DF"), A("SHU", 0, 64), A("IDF", 0, 64), OP.subtract)
-        ts(A("TE", 128, 192), A("TE", 0, 64), -1.0, None, OP.is_equal)
-        tt(A("DF"), A("DF"), A("IDF", 0, 64), OP.subtract)
-        tt(A("DF"), A("DF"), A("TE", 128, 192), OP.add)
-        fill(A("DF", 0, 1, 1, 0, 1), -1.0)
         ts(A("MROW", 0, 128), A("MROW", 0, 128), 1.0, None, OP.min)
-        fill(A("ONE"), 1.0)
         ts(A("ATK"), A("AT1"), -1.0, 1.0, OP.add, OP.max)
         ts(A("ATK"), A("ATK"), 4096.0, None, OP.mult)
         fill(A("HM"), 0.0)
@@ -278,6 +271,12 @@ def rank_program(g, core, T, topo):
             ts(A(ht), A("KEX"), pc(7), float(ha), OP.add, OP.add)
             rows(name, 0, 0, A(lt))
             rows(name, 0, 1, A(ht))
+
+    def st2():
+        ts(pc(6), pc(0), 0.0, 64.0, OP.is_equal, OP.mult)
+        ts(pc(8), pc(0), 1.0, 64.0, OP.is_equal, OP.mult)
+        tt(pc(6), pc(6), pc(8), OP.subtract)
+        ts(A("ST2"), A("VT2", 3072, 4096), pc(6), None, OP.add)
 
     zb = lambda k: A("ZB", 0, k)
     half = lambda nm, h: A(nm, 128 * h, 128 * h + 128)
@@ -317,7 +316,7 @@ def rank_program(g, core, T, topo):
         tt(A("DLO"), A("TD"), A("DHI"), OP.subtract)
         rows("KT", 0, 4, A("DLO"), "y")
         for h in range(2):
-            cp(half("VL", h), A("SL0", 256 * t + 128 * h, 256 * t + 128 * h + 128))
+            cp(half("VL", h), half("HI", h))
         tt(A("TC"), A("TD"), A("AT1"), OP.add)
         ts(A("BLB"), A("TC"), 15.0, None, OP.add)
         ts(A("ELB"), A("EB", 0, 256), -1.0, None, OP.add)
@@ -349,36 +348,39 @@ def rank_program(g, core, T, topo):
         def relist(h):
             cp(half("VL", h), A("P%d" % (4 + h), 0, 128))
 
-        for s in range(4):
+        for h in range(2):
+            exts("KT", 0, h, "P%d" % (4 + h), S_B)
+        kid(0)
+        xa(0)
+        xa(1)
+        for h in range(2):
+            ts(half("TD", h), A("P%d" % (4 + h), 0, 128), 16.0, None, OP.add)
+            tr(A("P%d" % (6 + h), 0, 128), half("TD", h))
+        ts(A("KEY"), A("EB", 0, 256), 4096.0, None, OP.mult)
+        tt(A("KEY"), A("KEY"), A("AT1"), OP.subtract)
+        for h in (1, 0):
+            cp(half("BLW", h), A("P%d" % (6 + h), 0, 128))
+        act(A("XB", 2048, 4096), IND(X, 0, 4112, "BLW", 128, 256))
+        kid(1)
+        cp(A("XB", 0, 2048), IND(X, 0, 4112, "BLW", 0, 128))
+        xb(0)
+        xb(1)
+        small(0, False)
+        tt(A("KEY"), A("KEY"), A("NHB"), OP.mult)
+        ts(A("HMB"), A("NHB"), -BIG, BIG, OP.mult, OP.add)
+        for q in range(8):
+            dma(A("HM", 66 * q, 66 * q + 64, 1, 0, 64), A("HMB", 0, 256, 1, 16 * q, 16 * q + 16))
+        iota(A("WB", 0, 4096), [[0, 4096]], 0, 0)
+        iota(A("WF", 0, 4096), [[0, 4096]], 0, 0)
+        relist(0)
+        for s in range(1, 4):
             xa(0)
-            if s == 0:
-                for h in range(2):
-                    exts("KT", 0, h, "P%d" % (4 + h), S_B)
-                for h in range(2):
-                    ts(half("TD", h), A("P%d" % (4 + h), 0, 128), 16.0, None, OP.add)
-                    tr(A("P%d" % (6 + h), 0, 128), half("TD", h))
-                for h in (1, 0):
-                    cp(half("BLW", h), A("P%d" % (6 + h), 0, 128))
-                act(A("XB", 2048, 4096), IND(X, 0, 4112, "BLW", 128, 256))
-                cp(A("XB", 0, 2048), IND(X, 0, 4112, "BLW", 0, 128))
-                kid(0)
-            else:
-                kid(0)
-                small(1, False)
+            kid(0)
+            small(1, False)
             xb(0)
-            if s > 0:
-                relist(1)
+            relist(1)
             xa(1)
             kid(1)
-            if s == 0:
-                ts(A("KEY"), A("EB", 0, 256), 4096.0, None, OP.mult)
-                tt(A("KEY"), A("KEY"), A("AT1"), OP.subtract)
-                tt(A("KEY"), A("KEY"), A("NHB"), OP.mult)
-                ts(A("HMB"), A("NHB"), -BIG, BIG, OP.mult, OP.add)
-                for q in range(8):
-                    dma(A("HM", 66 * q, 66 * q + 64, 1, 0, 64), A("HMB", 0, 256, 1, 16 * q, 16 * q + 16))
-                iota(A("WB", 0, 4096), [[0, 4096]], 0, 0)
-                iota(A("WF", 0, 4096), [[0, 4096]], 0, 0)
             if s == 1:
                 act(half("HIT", 0), A("P2", 256, 384))
                 act(half("HIT", 1), A("P3", 256, 384))
@@ -386,35 +388,44 @@ def rank_program(g, core, T, topo):
             xb(1)
             if s < 3:
                 relist(0)
-            if s in (1, 2):
                 o = 4112 if s == 1 else 8208
                 act(A(X, o, o + 4096), A(X, 15, 4111), AF.Relu, pc(9 + s))
 
-        mm(A("P6", 0, 264, 1, 0, 64), zb(64), zb(264), True, False)
-        mm(A("P7", 0, 264, 1, 0, 64), zb(64), zb(264), True, False)
-        slot = 0
+        for b in range(4, 8):
+            mm(A("P%d" % b, 0, 264, 1, 0, 65), zb(65), zb(264), True, False)
+        slot, slot2 = 0, 0
         for h in range(2):
             if h == 1:
                 small(1, True)
             ts(half("HI", h), half("VI", h), 6, None, OP.arith_shift_right)
-            ts(half("LI", h), half("VI", h), 63, None, OP.bitwise_and)
             ts(half("TA", h), half("HI", h), -64.0, None, OP.add)
-            ts(half("S2", h), half("LI", h), 1.0, None, OP.add)
+            ts(half("HI", h), half("VI", h), 63, None, OP.bitwise_and)
+            ts(half("S2", h), half("HI", h), 1.0, None, OP.add)
             tt(half("S1", h), half("TA", h), half("HIT", h), OP.mult)
             for q in range(8):
                 for i in range(16):
                     c = 128 * h + 16 * q + i
-                    o = 130 * (slot % 94)
-                    slot += 1
-                    ts(A(XO, o, o + 130), A("CR"), A("S1", c, c + 1), A("S2", c, c + 1), OP.max, OP.min)
-                    mm(A("P%d" % (6 + q // 4), 66 * (q % 4), 66 * (q % 4) + 66, 1, 0, 64), A(XO, o, o + 64),
-                       A(XO, o + 64, o + 130), False, h == 1 and i == 15 and q % 4 == 3)
-        act(A("SC", 0, 264), A("P6", 0, 264, 1, 0, 64))
-        cp(A("SC", 264, 528), A("P7", 0, 264, 1, 0, 64))
+                    if i % 4 == 3:
+                        o, b, last = 7860 + 131 * (slot2 % 30), 4, 15
+                        slot2 += 1
+                        act(A(XO, o, o + 65), A("CR", 0, 65), AF.Relu, A("S1", c, c + 1), -1.0)
+                        act(A(XO, o + 65, o + 131), A("CR", 65, 131), AF.Relu, A("S2", c, c + 1), -1.0)
+                    else:
+                        o, b, last = 131 * (slot % 60), 6, 14
+                        slot += 1
+                        ts(A(XO, o, o + 131), A("CR", 0, 131), A("S1", c, c + 1), A("S2", c, c + 1), OP.max, OP.min)
+                    mm(A("P%d" % (b + q // 4), 66 * (q % 4), 66 * (q % 4) + 66, 1, 0, 65), A(XO, o, o + 65),
+                       A(XO, o + 65, o + 131), False, h == 1 and i == last and q % 4 == 3)
+        if t == 0:
+            dma(A("HI"), IO("start", slice(0, 128), slice(256, 512)), "y")
+        act(A("SC", 0, 264), A("P6", 0, 264, 1, 0, 65))
+        cp(A("SC", 264, 528), A("P7", 0, 264, 1, 0, 65))
+        tt(A("SC", 264, 528), A("SC", 264, 528), A("P5", 0, 264, 1, 0, 65), OP.subtract)
+        tt(A("SC", 0, 264), A("SC", 0, 264), A("P4", 0, 264, 1, 0, 65), OP.subtract)
         tt(A("D1", 0, 527), A("SC", 1, 528), A("SC", 0, 527), OP.subtract)
         tt(A("SC", 0, 526), A("D1", 0, 526), A("D1", 1, 527), OP.subtract)
         for b, (c0, c1) in enumerate(((0, 264), (264, 526))):
-            mm(A("P%d" % (6 + b), 0, c1 - c0, 1, 0, 64), A("DF", 0, 64, 1, 0, 64), A("SC", c0, c1))
+            mm(A("P%d" % (6 + b), 0, c1 - c0, 1, 0, 64), A("DF", 0, 64, 1, 0, 65), A("SC", c0, c1))
             tt(A("FL", c0, c1), A("P%d" % (6 + b), 0, c1 - c0, 1, 0, 64), A("HM", c0, c1, 1, 0, 64), OP.mult)
         for q in range(8):
             dma(A(XO, 15, 4111, 1, 16 * q, 16 * q + 1), A("FL", 66 * q, 66 * q + 64), "y" if q % 2 else "s")
@@ -425,6 +436,8 @@ def rank_program(g, core, T, topo):
         cp(A(XO, GB + 2048, GB + 4096), IND(XO, 0, 4112, "BLB", 128, 256))
         for h in range(2):
             exts(XO, GB, h, "P%d" % h, S_0)
+        if t == 0:
+            st2()
         ts(A("KEEP"), A("HB"), 0.0, None, OP.is_le)
         fill(A("TE"), 0.0)
         scan(A("TA"), A("KEEP"), A("TE"), OP.add, OP.add)
@@ -454,7 +467,6 @@ def rank_program(g, core, T, topo):
         rows(XO, KM, 3, A("DLO"), "y")
         for h in range(2):
             act(A(XO, GB + 2048 * h, GB + 2048 * h + 2048), IND(XO, KM, KM + 4096, "ELB", 128 * h, 128 * h + 128))
-            exts(XO, GB, h, "P%d" % h, S_K, 16)
         tt(A("IEX"), A("TA"), A("KI"), OP.subtract)
         tt(A("TB"), A("TOP"), A("IEX"), OP.mult)
         scan(A("IH"), A("TB"), A("TB"), OP.max, OP.max)
@@ -476,7 +488,8 @@ def rank_program(g, core, T, topo):
         tt(A("TB"), A("TB"), A("KI"), OP.mult)
         tt(A("Q0M"), A("TB"), A("TD"), OP.add)
         ts(A("TE"), A("INS"), -2.0, 2.0, OP.mult, OP.add)
-        sc0(1)
+        for h in range(2):
+            exts(XO, GB, h, "P%d" % h, S_K, 16)
         for h in range(2):
             cp(half("TA", h), A("P%d" % h, 128, 256))
             tr(A("P2", 128 * h, 128 * h + 128), half("TA", h))
@@ -500,9 +513,10 @@ def rank_program(g, core, T, topo):
         tt(A("TA"), A("P3", 0, 256), A("KEX"), OP.subtract)
         tt(A("TA"), A("TA"), A("TD"), OP.add)
         split(A("PHI"), A("PLO"), A("TA"))
-        sc0(2)
-        sc0(3)
-        for k in range(4):
+        act(IND("WF", 0, 16384, "QL2", 192, 256), A("ST2"), AF.Silu)
+        for k in range(1, 4):
+            sc0(k)
+        for k in range(3):
             sc2(k)
         for k in range(3):
             o = 4096 + (15, 4112, 8208)[k]
@@ -512,8 +526,10 @@ def rank_program(g, core, T, topo):
         act(A("XB", 0, 2048), A("WF", 0, 2048))
         for h in (1, 0):
             mm(A("P%d" % h, 0, 128), zb(128), zb(128), True, False)
-            exts("WB", 0, h, "P%d" % h, S_01, 8, False, False)
-            exts("XB", 0, h, "P%d" % h, S_01, 8, False, "last")
+            exts("XB", 0, h, "P%d" % h, S_01, 8, False, False)
+        for h in (1, 0):
+            exts("WB", 0, h, "P%d" % h, S_01, 8, False, "last")
+        for h in (1, 0):
             ts(half("TB", h), A("P%d" % h, 0, 128), 15.0, None, OP.add)
             tr(A("P%d" % (2 + h), 0, 128), half("TB", h))
             cp(half("VL", h), A("P%d" % (2 + h), 0, 128))

from concourse.mybir import dt, AluOpType, AxisListType, ActivationFunctionType

OP = AluOpType
AF = ActivationFunctionType
F32, BF, I32, U16 = "float32", "bfloat16", "int32", "uint16"
NDMA = 110
SCRATCH = {
    "XW0": ("sbuf", [128, 12304], BF), "XW1": ("sbuf", [128, 12304], BF),
    "XB": ("sbuf", [128, 4096], BF), "W": ("sbuf", [128, 4096], BF), "KT": ("sbuf", [128, 4096], BF),
    "WB": ("sbuf", [128, 16416], BF), "WF": ("sbuf", [128, 16384], F32),
    "VT0": ("sbuf", [128, 4096], BF), "VT2": ("sbuf", [128, 4096], BF), "ST1": ("sbuf", [128, 4096], F32),
    "ST2": ("sbuf", [128, 1024], F32),
    "ZB": ("sbuf", [128, 264], BF), "CR": ("sbuf", [128, 132], BF),
    "IDF": ("sbuf", [128, 128], F32), "SHU": ("sbuf", [128, 128], F32),
    "SHD": ("sbuf", [128, 128], F32), "TRI": ("sbuf", [128, 128], F32), "DF": ("sbuf", [128, 64], F32),
    "MROW": ("sbuf", [128, 128], F32), "ONE": ("sbuf", [128, 2], F32), "PI": ("sbuf", [128, 8], I32),
    "PC": ("sbuf", [128, 16], F32), "SEL": ("sbuf", [128, 128], BF),
    "AT1": ("sbuf", [128, 256], F32), "ATK": ("sbuf", [128, 256], F32), "QT": ("sbuf", [128, 256], F32),
    "EB": ("sbuf", [128, 258], F32),
    "NHB": ("sbuf", [128, 256], BF), "DHI": ("sbuf", [128, 256], BF), "DLO": ("sbuf", [128, 256], BF),
    "HMB": ("sbuf", [128, 256], BF), "HM": ("sbuf", [128, 528], BF),
    "BLB": ("sbuf", [128, 256], U16), "ELB": ("sbuf", [128, 256], U16), "BLW": ("sbuf", [128, 256], U16),
    "VL": ("sbuf", [128, 256], U16), "QL0": ("sbuf", [128, 256], U16), "QL1": ("sbuf", [128, 256], U16),
    "QL2": ("sbuf", [128, 256], U16),
    "TA": ("sbuf", [128, 256], F32), "TB": ("sbuf", [128, 256], F32), "TC": ("sbuf", [128, 256], F32),
    "TD": ("sbuf", [128, 256], F32), "TE": ("sbuf", [128, 256], F32),
    "VI": ("sbuf", [128, 256], I32), "HI": ("sbuf", [128, 256], I32),
    "S1": ("sbuf", [128, 256], BF), "S2": ("sbuf", [128, 256], BF), "FL": ("sbuf", [64, 528], BF),
    "HB": ("sbuf", [128, 256], BF), "HB1": ("sbuf", [128, 256], BF),
    "KEEP": ("sbuf", [128, 256], BF), "KEX": ("sbuf", [128, 256], F32), "R": ("sbuf", [128, 256], F32),
    "INS": ("sbuf", [128, 256], BF), "KI": ("sbuf", [128, 256], BF), "IEX": ("sbuf", [128, 256], F32),
    "IH": ("sbuf", [128, 256], F32), "TOP": ("sbuf", [128, 256], BF),
    "PHI": ("sbuf", [128, 256], BF), "PLO": ("sbuf", [128, 256], BF),
    "CROW": ("sbuf", [128, 128], F32), "TX": ("sbuf", [128, 256], BF),
    "LX0": ("sbuf", [128, 256], BF), "LX1": ("sbuf", [128, 256], BF),
    "ES0": ("sbuf", [128, 16], F32), "ES1": ("sbuf", [128, 16], F32),
    "RE0": ("sbuf", [128, 16], F32), "RE1": ("sbuf", [128, 16], F32),
}
for _k in range(8):
    SCRATCH["P%d" % _k] = ("psum", [128, 512], F32)
SEMAPHORES = ["qv", "qs", "qt", "qg"] + ["d%d" % k for k in range(NDMA)]
SEMAPHORES += ["%s%d" % (a, k) for a in ("xs", "xr", "es", "er") for k in range(2)]

ALIAS = {"SC": (4096, 528, 65), "D1": (4640, 528, 65), "HIT": (5200, 256, 128), "KEY": (5456, 256, 128),
         "Q0M": (5712, 256, 128)}
S_P, S_M, S_A, S_D, S_N, S_B, S_0, S_01, S_K, S_I = 0, 8, 16, 24, 32, 40, 48, 56, 64, 72
BIG = float(2 ** 24)
KM, GB = 4112, 8208


def rank_program(g, core, T, topo):
    rank = T.rank_of(core)
    if rank is None:
        return
    n = len(T.cores)
    nxt, prv = T.cores[(rank + 1) % n], T.cores[(rank - 1) % n]
    eng = {"v": g.vector, "s": g.scalar, "t": g.tensor, "g": g, "y": g.sync}
    hist, known, cnt, total = {}, {q: {} for q in eng}, {q: 0 for q in eng}, {}
    nd, serial = [0], [0]

    def over(a, b):
        if a[0] >= b[1] or b[0] >= a[1] or a[3] >= b[4] or b[3] >= a[4]:
            return False
        return not (a[2] == 16 and b[2] == 16 and a[0] % 16 != b[0] % 16)

    def inside(a, b):
        if not (b[0] <= a[0] and a[1] <= b[1] and b[3] <= a[3] and a[4] <= b[4]):
            return False
        return b[2] == 1 or (a[2] == 16 and a[0] % 16 == b[0] % 16)

    def is_psum(name):
        return name[0] == "P" and name[1:].isdigit()

    def op(q, call, R, W, dma=False, remote=None):
        deps = []
        for name, reg in R:
            ps = is_psum(name)
            for r in hist.get(name, []):
                if over(r["reg"], reg) and (r["w"] or (ps and r["q"] != q)):
                    deps.append(r)
        for name, reg in W:
            for r in hist.get(name, []):
                if over(r["reg"], reg) and not (q == "t" and r["q"] == "t"):
                    deps.append(r)
        deps.sort(key=lambda r: -r["n"])
        kn = known[q]
        for r in deps:
            if kn.get(r["sem"], 0) >= r["val"]:
                continue
            eng[q].wait_ge(T.sem[r["sem"]], r["val"])
            for k, v in r["vc"].items():
                if kn.get(k, 0) < v:
                    kn[k] = v
            kn[r["sem"]] = r["val"]
        ins = call()
        serial[0] += 1
        if remote is not None:
            sem, val = remote
        elif dma:
            sem, val = "d%d" % nd[0], 16
            nd[0] += 1
            ins.then_inc(T.sem[sem], 16)
        else:
            cnt[q] += 1
            sem, val = "q" + q, cnt[q]
            ins.then_inc(T.sem[sem], 1)
        total[sem] = val
        vc = dict(kn)
        for w, lst in ((False, R), (True, W)):
            for name, reg in lst:
                h = hist.setdefault(name, [])
                if w or is_psum(name):
                    h[:] = [r for r in h if not inside(r["reg"], reg)]
                elif not dma and remote is None:
                    h[:] = [r for r in h if r["w"] or r["dma"] or r["q"] != q or not inside(r["reg"], reg)]
                h.append({"reg": reg, "w": w, "q": q, "sem": sem, "val": val, "vc": vc, "n": serial[0],
                          "dma": dma or remote is not None})

    def A(name, c0=0, c1=None, cs=1, p0=0, p1=None, ps=1):
        if name in ALIAS:
            o, k, r = ALIAS[name]
            return A("WF", o + c0, o + (k if c1 is None else c1), cs, p0, r if p1 is None else p1, ps)
        shape = T[name].shape
        c1 = shape[1] if c1 is None else c1
        p1 = shape[0] if p1 is None else p1
        sc = slice(c0, c1) if cs == 1 else slice(c0, c1, cs)
        sp = slice(p0, p1) if ps == 1 else slice(p0, p1, ps)
        reg = (0, 128, 1, 0, 512) if is_psum(name) else (p0, p1, ps, c0, c1)
        return T[name][sp, sc], [(name, reg)]

    def IND(name, c0, c1, lst, l0, l1):
        return (T[name][:, c0:c1].indirect(T[lst][:, l0:l1]),
                [(name, (0, 128, 1, c0, c1)), (lst, (0, 128, 1, l0, l1))])

    def outs(o):
        return o[1][:1], o[1][1:]

    def tt(o, a, b, f):
        op("v", lambda: g.vector.tensor_tensor(o[0], a[0], b[0], f), a[1] + b[1], o[1])

    def ts(o, a, s1, s2, f1, f2=None):
        r = list(a[1])
        x = [s1, s2]
        for k in range(2):
            if isinstance(x[k], tuple):
                r += x[k][1]
                x[k] = x[k][0]
        if f2 is None:
            op("v", lambda: g.vector.tensor_scalar(o[0], a[0], x[0], None, f1), r, o[1])
        else:
            op("v", lambda: g.vector.tensor_scalar(o[0], a[0], x[0], x[1], f1, f2), r, o[1])

    def cp(o, a):
        w, r = outs(o)
        op("v", lambda: g.vector.tensor_copy(o[0], a[0]), a[1] + r, w)

    def fill(o, val):
        op("v", lambda: g.vector.memset(o[0], val), [], o[1])

    def scan(o, a, b, f1, f2):
        op("v", lambda: g.vector.tensor_tensor_scan(o[0], a[0], b[0], 0.0, f1, f2), a[1] + b[1], o[1])

    def act(o, a, f=AF.Copy, bias=None, scale=1.0):
        w, r = outs(o)
        if bias is None:
            op("s", lambda: g.scalar.activation(o[0], a[0], f), a[1] + r, w)
        else:
            op("s", lambda: g.scalar.activation(o[0], a[0], f, bias=bias[0], scale=scale), a[1] + r + bias[1], w)

    def mm(o, l, r, start=True, stop=True):
        op("t", lambda: g.tensor.matmul(o[0], l[0], r[0], start, stop), l[1] + r[1], o[1])

    def dma(o, a, q="y"):
        op(q, lambda: eng[q].dma_start(o[0], a[0]), a[1], o[1], dma=True)

    def iota(o, pattern, base, mul, loose=True):
        if loose:
            op("g", lambda: g.iota(o[0], pattern, base, mul, allow_small_or_imprecise_dtypes=True), [], o[1])
        else:
            op("g", lambda: g.iota(o[0], pattern, base, mul), [], o[1])

    def IO(name, *idx):
        return (T[name][idx] if idx else T[name][:]), []

    def sel(c, k=8):
        return A("SEL", c, c + k)

    def tr(o, a):
        mm(o, a, A("IDF"))

    def rows(name, off, r, src, q="y"):
        dma(A(name, off, off + 4096, 1, r, 128, 16), src, q)

    dma(A("VI"), IO("ends"), "y")
    dma(A("HI"), IO("start", slice(0, 128), slice(0, 256)), "s")
    fill(A("XW0", 0, 16), 0.0)
    fill(A("XW0", 4104, 4112), 0.0)
    dma(A("XW0", 15, 4111), IO("x"), "y")
    dma(A("W"), IO("w"), "s")

    def pick(o, pattern, f, v, base, mul):
        op("g", lambda: g.affine_select(o[0], o[0], pattern, f, v, base, mul), o[1], o[1])

    def selector(c, lo, hi):
        pick(sel(c), [[-16, 8]], OP.is_ge, 0.0, -lo, 1)
        pick(sel(c), [[16, 8]], OP.is_ge, 0.0, hi, -1)

    def one_group(nm):
        pick(A(nm), [[-16, 8], [0, 16]], OP.is_ge, 0.0, 0, 1)
        pick(A(nm), [[16, 8], [0, 16]], OP.is_ge, 0.0, 15, -1)

    for nm, v in (("SHU", 0.0), ("SEL", 1.0), ("IDF", 0.0), ("SHD", 0.0), ("TRI", 1.0), ("DF", 0.0)):
        fill(A(nm), v)
    fill(sel(S_M), -1.0)
    fill(A("ZB"), 0.0)
    fill(A("ONE"), 1.0)
    fill(A("KT"), 0.0)
    iota(A("PI", 0, 1), [[0, 1]], 0, 1, False)
    iota(A("TA"), [[1, 256]], 0, 0)
    iota(A("TB"), [[0, 2], [1, 128]], 0, 0)
    iota(A("TC"), [[128, 2], [0, 128]], 0, 0)
    pick(A("SHU"), [[-1, 128]], OP.not_equal, 1.0, -1, 1)
    for c, lo, hi in ((S_B, 0, 4), (S_P, 0, 15), (S_M, 0, 15), (S_A, 0, 2), (S_D, 3, 4), (S_N, 2, 2)):
        selector(c, lo, hi)
    pick(sel(S_B), [[-16, 8]], OP.not_equal, 0.0, -2, 1)
    pick(A("IDF"), [[-1, 128]], OP.not_equal, 1.0, 0, 1)
    iota(A("CR", 0, 65), [[1, 65]], -65, 0)
    iota(A("CR", 65, 131), [[1, 66]], 0, 0)
    iota(A("QT"), [[128, 2], [0, 8], [256, 16]], 0, 1)
    iota(A("MROW", 0, 128), [[0, 8], [1, 16]], 0, 0)
    iota(A("KEX"), [[0, 16], [256, 16]], 0, 0)
    iota(A("IEX"), [[1, 16], [0, 16]], 0, 0)
    pi = lambda k: A("PI", k, k + 1)
    pc = lambda k: A("PC", k, k + 1)
    ts(pi(1), pi(0), 15, None, OP.bitwise_and)
    ts(pi(3), pi(0), 7, None, OP.bitwise_and)
    cp(pc(0), pi(1))
    ts(pc(1), pc(0), 256.0, None, OP.mult)
    ts(A("AT1"), A("TA"), pc(1), 1.0, OP.add, OP.add)
    cp(A("PLO"), A("TB"))
    ts(A("PHI"), A("TC"), pc(1), None, OP.add)
    rows("KT", 0, 0, A("PLO"), "y")
    rows("KT", 0, 1, A("PHI"), "s")
    ts(pc(5), pc(0), 15.0, 8192.0, OP.is_equal, OP.mult)

    def late_constants():
        for c, lo, hi in ((S_0, 0, 0), (S_01, 0, 1), (S_K, 0, 1), (S_I, 2, 3)):
            selector(c, lo, hi)
        pick(A("SHD"), [[-1, 128]], OP.not_equal, 1.0, 1, 1)
        one_group("SHD")
        pick(A("TRI"), [[1, 128]], OP.is_ge, 0.0, -1, -1)
        one_group("TRI")
        for k, v in ((0, 1.0), (1, -2.0), (2, 1.0)):
            pick(A("DF"), [[-1, 64]], OP.not_equal, v, -k, 1)
        fill(pc(10), -1.0)
        fill(pc(11), -2.0)
        ts(A("MROW", 0, 128), A("MROW", 0, 128), 1.0, None, OP.min)
        ts(A("ATK"), A("AT1"), -1.0, 1.0, OP.add, OP.max)
        ts(A("ATK"), A("ATK"), 4096.0, None, OP.mult)
        fill(A("HM"), 0.0)
        fill(A("WB", 16384, 16416), 0.0)
        cp(pc(3), pi(3))
        ts(pc(4), pc(3), 16.0, None, OP.mult)
        tt(pc(7), pc(0), pc(3), OP.subtract)
        ts(pc(7), pc(7), 16.0, None, OP.mult)
        for name in ("VT0", "ST1", "VT2"):
            iota(A(name), [[0, 4096]], 0, 0)
        for name, la, ha, lt, ht in (("VT0", 0, 0, "PLO", "PHI"), ("ST1", 65, 4032, "R", "IH"),
                                     ("VT2", 1, 8192, "HB", "HB1")):
            ts(A(lt), A("IEX"), pc(4), float(la), OP.add, OP.add)
            ts(A(ht), A("KEX"), pc(7), float(ha), OP.add, OP.add)
            rows(name, 0, 0, A(lt))
            rows(name, 0, 1, A(ht))

    def st2():
        ts(pc(6), pc(0), 0.0, 64.0, OP.is_equal, OP.mult)
        ts(pc(8), pc(0), 1.0, 64.0, OP.is_equal, OP.mult)
        tt(pc(6), pc(6), pc(8), OP.subtract)
        ts(A("ST2"), A("VT2", 3072, 4096), pc(6), None, OP.add)

    zb = lambda k: A("ZB", 0, k)
    half = lambda nm, h: A(nm, 128 * h, 128 * h + 128)

    def exts(buf, off, h, out, s, k=8, start=True, stop=True):
        for i in range(16):
            mm(A(out, i, i + (k - 1) * 16 + 1, 16), A(buf, off + 2048 * h + i, off + 2048 * h + 2048, 16), sel(s, k),
               start, stop if stop is True else (stop == "last" and i == 15))

    def maxcarry(col):
        mm(A("P4", 0, 128, 1, 0, 1), col, A("SHD"))
        scan(A("CROW", 0, 128, 1, 0, 1), A("MROW", 0, 128, 1, 0, 1), A("P4", 0, 128, 1, 0, 1), OP.mult, OP.max)
        mm(A("P5", 0, 1), A("CROW", 0, 128, 1, 0, 1), A("ONE", 0, 1, 1, 0, 1))
        return A("P5", 0, 1)

    def sumcarry(col):
        mm(A("P5", 8, 9), A("TRI"), col)
        return A("P5", 8, 9)

    def split(hi, lo, src):
        cp(hi, src)
        tt(lo, src, hi, OP.subtract)

    for t in range(2):
        X, XO = "XW%d" % t, "XW%d" % (1 - t)
        if t == 0:
            cp(A("EB", 0, 256), A("VI"))
        mm(A("P4", 0, 1), A("SHU"), A("EB", 0, 1))
        tt(A("NHB"), A("EB", 0, 256), A("AT1"), OP.is_gt)
        rows("KT", 0, 2, A("NHB"), "y")
        ts(A("EB", 256, 257), A("P4", 0, 1), pc(5), None, OP.add)
        tt(A("TC"), A("EB", 1, 257), A("EB", 0, 256), OP.is_lt)
        tt(A("TD"), A("EB", 1, 257), A("AT1"), OP.subtract)
        tt(A("TD"), A("TD"), A("TC"), OP.mult)
        cp(A("DHI"), A("TD"))
        rows("KT", 0, 3, A("DHI"), "s")
        tt(A("DLO"), A("TD"), A("DHI"), OP.subtract)
        rows("KT", 0, 4, A("DLO"), "y")
        for h in range(2):
            cp(half("VL", h), half("HI", h))
        tt(A("TC"), A("TD"), A("AT1"), OP.add)
        ts(A("BLB"), A("TC"), 15.0, None, OP.add)
        ts(A("ELB"), A("EB", 0, 256), -1.0, None, OP.add)
        if t == 0:
            late_constants()

        def xa(h):
            tt(A("WB", 4096 + 2048 * h, 6144 + 2048 * h), IND(X, 16, 4112, "VL", 128 * h, 128 * h + 128),
               A("W", 2048 * h, 2048 * h + 2048), OP.min)
            mm(A("P%d" % h, 0, 128), zb(128), zb(128), True, False)
            exts("WB", 4096, h, "P%d" % h, S_P, 8, False, False)

        def xb(h):
            tt(A("WB", 8192 + 2048 * h, 10240 + 2048 * h), IND("XB", 0, 4096, "VL", 128 * h, 128 * h + 128),
               A("W", 2048 * h, 2048 * h + 2048), OP.min)
            exts("WB", 8192, h, "P%d" % h, S_M, 8, False, "last")

        def kid(h):
            act(A("WB", 12288 + 2048 * h, 14336 + 2048 * h), IND("KT", 0, 4096, "VL", 128 * h, 128 * h + 128))
            exts("WB", 12288, h, "P%d" % (2 + h), S_A, 24)

        def small(h, last):
            ts(half("TA", h), A("P%d" % h, 0, 128), 0.0, None, OP.is_gt)
            tt(half("TB", h), A("P%d" % (2 + h), 128, 256), half("TA", h), OP.mult)
            tt(half("VI" if last else "TC", h), A("P%d" % (2 + h), 0, 128), half("TB", h), OP.add)
            if not last:
                tr(A("P%d" % (4 + h), 0, 128), half("TC", h))

        def relist(h):
            cp(half("VL", h), A("P%d" % (4 + h), 0, 128))

        for h in range(2):
            exts("KT", 0, h, "P%d" % (4 + h), S_B)
        kid(0)
        xa(0)
        xa(1)
        for h in range(2):
            ts(half("TD", h), A("P%d" % (4 + h), 0, 128), 16.0, None, OP.add)
            tr(A("P%d" % (6 + h), 0, 128), half("TD", h))
        ts(A("KEY"), A("EB", 0, 256), 4096.0, None, OP.mult)
        tt(A("KEY"), A("KEY"), A("AT1"), OP.subtract)
        for h in (1, 0):
            cp(half("BLW", h), A("P%d" % (6 + h), 0, 128))
        act(A("XB", 2048, 4096), IND(X, 0, 4112, "BLW", 128, 256))
        kid(1)
        cp(A("XB", 0, 2048), IND(X, 0, 4112, "BLW", 0, 128))
        xb(0)
        xb(1)
        small(0, False)
        tt(A("KEY"), A("KEY"), A("NHB"), OP.mult)
        ts(A("HMB"), A("NHB"), -BIG, BIG, OP.mult, OP.add)
        for q in range(8):
            dma(A("HM", 66 * q, 66 * q + 64, 1, 0, 64), A("HMB", 0, 256, 1, 16 * q, 16 * q + 16))
        iota(A("WB", 0, 4096), [[0, 4096]], 0, 0)
        iota(A("WF", 0, 4096), [[0, 4096]], 0, 0)
        relist(0)
        for s in range(1, 4):
            xa(0)
            kid(0)
            small(1, False)
            xb(0)
            relist(1)
            xa(1)
            kid(1)
            if s == 1:
                act(half("HIT", 0), A("P2", 256, 384))
                act(half("HIT", 1), A("P3", 256, 384))
            small(0, s == 3)
            xb(1)
            if s < 3:
                relist(0)
                o = 4112 if s == 1 else 8208
                act(A(X, o, o + 4096), A(X, 15, 4111), AF.Relu, pc(9 + s))

        for b in range(4, 8):
            mm(A("P%d" % b, 0, 264, 1, 0, 65), zb(65), zb(264), True, False)
        slot, slot2 = 0, 0
        for h in range(2):
            if h == 1:
                small(1, True)
            ts(half("HI", h), half("VI", h), 6, None, OP.arith_shift_right)
            ts(half("TA", h), half("HI", h), -64.0, None, OP.add)
            ts(half("HI", h), half("VI", h), 63, None, OP.bitwise_and)
            ts(half("S2", h), half("HI", h), 1.0, None, OP.add)
            tt(half("S1", h), half("TA", h), half("HIT", h), OP.mult)
            for q in range(8):
                for i in range(16):
                    c = 128 * h + 16 * q + i
                    if i % 4 == 3:
                        o, b, last = 7860 + 131 * (slot2 % 30), 4, 15
                        slot2 += 1
                        act(A(XO, o, o + 65), A("CR", 0, 65), AF.Relu, A("S1", c, c + 1), -1.0)
                        act(A(XO, o + 65, o + 131), A("CR", 65, 131), AF.Relu, A("S2", c, c + 1), -1.0)
                    else:
                        o, b, last = 131 * (slot % 60), 6, 14
                        slot += 1
                        ts(A(XO, o, o + 131), A("CR", 0, 131), A("S1", c, c + 1), A("S2", c, c + 1), OP.max, OP.min)
                    mm(A("P%d" % (b + q // 4), 66 * (q % 4), 66 * (q % 4) + 66, 1, 0, 65), A(XO, o, o + 65),
                       A(XO, o + 65, o + 131), False, h == 1 and i == last and q % 4 == 3)
        if t == 0:
            dma(A("HI"), IO("start", slice(0, 128), slice(256, 512)), "y")
        act(A("SC", 0, 264), A("P6", 0, 264, 1, 0, 65))
        cp(A("SC", 264, 528), A("P7", 0, 264, 1, 0, 65))
        tt(A("SC", 264, 528), A("SC", 264, 528), A("P5", 0, 264, 1, 0, 65), OP.subtract)
        tt(A("SC", 0, 264), A("SC", 0, 264), A("P4", 0, 264, 1, 0, 65), OP.subtract)
        tt(A("D1", 0, 527), A("SC", 1, 528), A("SC", 0, 527), OP.subtract)
        tt(A("SC", 0, 526), A("D1", 0, 526), A("D1", 1, 527), OP.subtract)
        for b, (c0, c1) in enumerate(((0, 264), (264, 526))):
            mm(A("P%d" % (6 + b), 0, c1 - c0, 1, 0, 64), A("DF", 0, 64, 1, 0, 65), A("SC", c0, c1))
            tt(A("FL", c0, c1), A("P%d" % (6 + b), 0, c1 - c0, 1, 0, 64), A("HM", c0, c1, 1, 0, 64), OP.mult)
        for q in range(8):
            dma(A(XO, 15, 4111, 1, 16 * q, 16 * q + 1), A("FL", 66 * q, 66 * q + 64), "y" if q % 2 else "s")
        dma(A("HB"), A(XO, 15, 4111, 1, 0, 128, 16), "y")
        dma(A("HB1"), A(XO, 16, 4112, 1, 0, 128, 16), "y")

        act(A(XO, GB, GB + 2048), IND(XO, 0, 4112, "BLB", 0, 128))
        cp(A(XO, GB + 2048, GB + 4096), IND(XO, 0, 4112, "BLB", 128, 256))
        for h in range(2):
            exts(XO, GB, h, "P%d" % h, S_0)
        if t == 0:
            st2()
        ts(A("KEEP"), A("HB"), 0.0, None, OP.is_le)
        fill(A("TE"), 0.0)
        scan(A("TA"), A("KEEP"), A("TE"), OP.add, OP.add)
        k0 = sumcarry(A("TA", 255, 256))
        for h in range(2):
            ts(half("TB", h), A("P%d" % h, 0, 128), 0.0, BIG, OP.is_gt, OP.mult)
            tr(A("P2", 128 * h, 128 * h + 128), half("TB", h))
        ts(A("TA"), A("TA"), k0, None, OP.add)
        split(A("PHI"), A("PLO"), A("TA"))
        rows(XO, KM, 0, A("PHI"), "y")
        rows(XO, KM, 1, A("PLO"), "y")
        tt(A("KEX"), A("TA"), A("KEEP"), OP.subtract)
        tt(A("TC"), A("P2", 0, 256), A("HB1"), OP.add)
        tt(A("TC"), A("TC"), A("KEY"), OP.min)
        scan(A("R"), A("TC"), A("TC"), OP.max, OP.max)
        c = maxcarry(A("R", 255, 256))
        ts(A("R"), A("R"), c, None, OP.max)
        tt(A("INS"), A("R"), A("ATK"), OP.is_ge)
        tt(A("KI"), A("KEEP"), A("INS"), OP.mult)
        scan(A("TA"), A("KI"), A("TE"), OP.add, OP.add)
        c = sumcarry(A("TA", 255, 256))
        tt(A("TOP"), A("R"), A("TC"), OP.is_equal)
        tt(A("TOP"), A("TOP"), A("INS"), OP.mult)
        ts(A("TA"), A("TA"), c, None, OP.add)
        split(A("DHI"), A("DLO"), A("TA"))
        rows(XO, KM, 2, A("DHI"), "y")
        rows(XO, KM, 3, A("DLO"), "y")
        for h in range(2):
            act(A(XO, GB + 2048 * h, GB + 2048 * h + 2048), IND(XO, KM, KM + 4096, "ELB", 128 * h, 128 * h + 128))
        tt(A("IEX"), A("TA"), A("KI"), OP.subtract)
        tt(A("TB"), A("TOP"), A("IEX"), OP.mult)
        scan(A("IH"), A("TB"), A("TB"), OP.max, OP.max)
        c = maxcarry(A("IH", 255, 256))
        ts(A("IH"), A("IH"), c, None, OP.max)
        tt(A("TB"), A("IH"), A("IEX"), OP.subtract)
        tt(A("TB"), A("TB"), A("INS"), OP.mult)
        tt(A("TB"), A("TB"), A("IEX"), OP.add)
        ts(A("TB"), A("TB"), 2.0, None, OP.mult)
        tt(A("TB"), A("TB"), A("KEX"), OP.add)
        ts(A("TD"), A("AT1"), 12287.0, None, OP.add)
        tt(A("TB"), A("TB"), A("TD"), OP.subtract)
        tt(A("TC"), A("TB"), A("KEEP"), OP.mult)
        tt(A("TC"), A("TC"), A("TD"), OP.add)
        cp(A("QL0"), A("TC"))
        sc0 = lambda k: cp(IND("WB", 0, 16384, "QL0", 64 * k, 64 * k + 64), A("VT0", 1024 * k, 1024 * k + 1024))
        sc2 = lambda k: cp(IND("WB", 0, 16384, "QL2", 64 * k, 64 * k + 64), A("VT2", 1024 * k, 1024 * k + 1024))
        sc0(0)
        tt(A("TB"), A("TB"), A("KI"), OP.mult)
        tt(A("Q0M"), A("TB"), A("TD"), OP.add)
        ts(A("TE"), A("INS"), -2.0, 2.0, OP.mult, OP.add)
        for h in range(2):
            exts(XO, GB, h, "P%d" % h, S_K, 16)
        for h in range(2):
            cp(half("TA", h), A("P%d" % h, 128, 256))
            tr(A("P2", 128 * h, 128 * h + 128), half("TA", h))
        for h in range(2):
            cp(half("TB", h), A("P%d" % h, 0, 128))
            tr(A("P3", 128 * h, 128 * h + 128), half("TB", h))
        tt(A("TC"), A("P2", 0, 256), A("TOP"), OP.mult)
        scan(A("R"), A("TC"), A("TC"), OP.max, OP.max)
        c = maxcarry(A("R", 255, 256))
        tt(A("TD"), A("P2", 0, 256), A("IEX"), OP.subtract)
        tt(A("TD"), A("TD"), A("TE"), OP.mult)
        ts(A("R"), A("R"), c, None, OP.max)
        tt(A("R"), A("R"), A("IH"), OP.subtract)
        tt(A("R"), A("R"), A("KI"), OP.mult)
        tt(A("TC"), A("Q0M"), A("R"), OP.add)
        cp(A("QL1"), A("TC"))
        for k in range(4):
            act(IND("WF", 0, 16384, "QL1", 64 * k, 64 * k + 64), A("ST1", 1024 * k, 1024 * k + 1024), AF.Silu)
        tt(A("TC"), A("TC"), A("R"), OP.add)
        cp(A("QL2"), A("TC"))
        tt(A("TA"), A("P3", 0, 256), A("KEX"), OP.subtract)
        tt(A("TA"), A("TA"), A("TD"), OP.add)
        split(A("PHI"), A("PLO"), A("TA"))
        act(IND("WF", 0, 16384, "QL2", 192, 256), A("ST2"), AF.Silu)
        for k in range(1, 4):
            sc0(k)
        for k in range(3):
            sc2(k)
        for k in range(3):
            o = 4096 + (15, 4112, 8208)[k]
            rows("WB", o, 0, A("PHI"), "y")
            rows("WB", o, 1, A("PLO"), "y")
        act(A("XB", 2048, 4096), A("WF", 2048, 4096))
        act(A("XB", 0, 2048), A("WF", 0, 2048))
        for h in (1, 0):
            mm(A("P%d" % h, 0, 128), zb(128), zb(128), True, False)
            exts("XB", 0, h, "P%d" % h, S_01, 8, False, False)
        for h in (1, 0):
            exts("WB", 0, h, "P%d" % h, S_01, 8, False, "last")
        for h in (1, 0):
            ts(half("TB", h), A("P%d" % h, 0, 128), 15.0, None, OP.add)
            tr(A("P%d" % (2 + h), 0, 128), half("TB", h))
            cp(half("VL", h), A("P%d" % (2 + h), 0, 128))
        LX, ES, RE = ["%s%d" % (nm, t) for nm in ("LX", "ES", "RE")]
        dx = 15 if t == 0 else 0
        SZ = lambda a, b: IND("WB", 4096, 16400, "VL", a, b)
        XI = lambda a, b: IND(X, 0, 12304, "VL", a, b)
        cp(A("TX"), XI(240, 256))
        act(A(XO, GB + 3840, GB + 4096), SZ(240, 256))
        for h in range(2):
            mm(A("P4", 8 * h, 8 * h + 8), A(XO, GB + 3840 + 128 * h, GB + 3968 + 128 * h), sel(S_01))
        tt(A(ES), A("P4", 0, 16), A("QT", 15, 256, 16), OP.add)
        ts(A(ES), A(ES), 4096.0, None, OP.min)
        rid, pid, _se = topo.addr(nxt)
        m = topo.mask(core, nxt)
        ne, nb = len(topo.engines(core, nxt)), len(topo.engines(prv, core))

        def send(src, dst, ss, rs):
            sa, da = A(src), T[dst][:]
            op("g", lambda: g.remote_dma(da, sa[0], T.sem[rs], T.sem[ss], pid, rid, m), sa[1], [], remote=(ss, ne))
            total[rs] = nb
            hist[dst] = [{"reg": (0, 128, 1, 0, 256), "w": True, "q": "remote", "sem": rs, "val": nb, "vc": {}, "n": 0,
                          "dma": True}]
        send("TX", LX, "xs%d" % t, "xr%d" % t)
        send(ES, RE, "es%d" % t, "er%d" % t)
        cp(A(XO, dx + 2048, dx + 3840), XI(128, 240))
        act(A(XO, GB + 2048, GB + 3840), SZ(128, 240))
        if t == 1:
            dma(IO("y", slice(0, 128), slice(2048, 3840)), A(XO, dx + 2048, dx + 3840))
        cp(A(XO, dx, dx + 2048), XI(0, 128))
        act(A(XO, GB, GB + 2048), SZ(0, 128))
        for i in list(range(8, 15)) + list(range(8)):
            for h in range(2):
                mm(A("P5", 128 * h + i, 128 * h + 113 + i, 16),
                   A(XO, GB + 256 * i + 128 * h, GB + 256 * i + 128 * h + 128), sel(S_01))
        for h in range(2):
            mm(A("P5", 128 * h + 15, 128 * h + 128, 16), zb(128), zb(8))
        if t == 0:
            cp(A(XO, 3855, 4111), A(LX))
        else:
            dma(IO("y", slice(0, 128), slice(0, 2048)), A(XO, dx, dx + 2048))
            dma(IO("y", slice(0, 128), slice(3840, 4096)), A(LX))
        tt(A("TA"), A("P5", 0, 256), A("QT"), OP.add)
        ts(A("TA"), A("TA"), 3840.0, None, OP.min)
        cp(A("TA", 15, 256, 16), A(RE))
        for h in range(2):
            tr(A("P6", 128 * h, 128 * h + 128), half("TA", h))
        cp(A("EB", 0, 256), A("P6", 0, 256))
        if t == 1:
            dma(IO("ye"), A("EB", 0, 256))

    for s in sorted(total):
        if known["g"].get(s, 0) < total[s]:
            g.wait_ge(T.sem[s], total[s])
